import numpy as np
import ml_dtypes


def mxq(x, axis, fmt="e4m3"):
    dtype, down = {"e4m3": (ml_dtypes.float8_e4m3fn, 7), "e5m2": (ml_dtypes.float8_e5m2, 14)}[fmt]
    v = np.moveaxis(np.asarray(x, np.float32).astype(ml_dtypes.bfloat16).astype(np.float64), axis, -1)
    blocks = v.reshape(v.shape[:-1] + (-1, 32))
    amax = np.abs(blocks).max(-1, keepdims=True)
    byte = np.maximum(np.where(amax > 0, np.frexp(amax)[1] - 1 + 127, 0) - down, 1)
    scale = np.exp2(byte - 127.0)
    codes = (blocks / scale).astype(np.float32).astype(dtype).astype(np.float64)
    return np.moveaxis((codes * scale).reshape(v.shape), -1, axis)


WIDE = False


def mx_kscale(k):
    if not WIDE:
        return np.ones(k)
    levels = np.array([10, -10, 5, -5, 0])
    if k % 512:
        return np.exp2(np.random.permutation(np.resize(levels, k // 32))).repeat(32)
    a = np.empty((k // 512, 16))
    for p in range(k // 512):
        a[p, :8] = np.random.permutation(np.resize(levels, 8))
        for g in range(8):
            far = levels[np.abs(levels - a[p, g]) >= 10]
            a[p, g + 8] = far[np.random.randint(len(far))]
    return np.exp2(a.ravel()).repeat(32)


def f64(x):
    return np.asarray(x).astype(np.float64)


def striped(idx):
    return np.tile(idx.reshape(-1, 16).T, (8, 1)).astype(np.uint16)


def unstriped(offs):
    return offs[:16].T.reshape(-1).astype(np.int64)


E2M1 = np.array([0.0, 0.5, 1.0, 1.5, 2.0, 3.0, 4.0, 6.0, -0.0, -0.5, -1.0, -1.5, -2.0, -3.0, -4.0, -6.0])


def pack_weight(w, fmt):
    k, n = w.shape
    w = f64(np.asarray(w, np.float32).astype(ml_dtypes.bfloat16)).reshape(k // 32, 32, n)
    amax = np.abs(w).max(1)
    if fmt == "e4m3":
        byte = np.frexp(amax)[1] - 1 + 127 - 7
    else:
        mant, ex = np.frexp(amax / 6.0)
        byte = np.where(mant > 0.5, ex, ex - 1) + 127
    byte = np.clip(np.where(amax > 0, byte, 1), 1, 254)
    scaled = (w * np.exp2(127.0 - byte)[:, None, :]).reshape(k, n).astype(np.float32)
    by_word = np.ascontiguousarray(scaled.reshape(k // 512, 128, 4, n).transpose(0, 1, 3, 2))
    if fmt == "e4m3":
        words = by_word.astype(ml_dtypes.float8_e4m3fn).view(np.uint8)
    else:
        c = by_word.astype(ml_dtypes.float4_e2m1fn).view(np.uint8) & 0xF
        words = (c[..., 0::2] | (c[..., 1::2] << 4)).reshape(k // 512, 128, 2 * n)
    return np.ascontiguousarray(words), np.ascontiguousarray(byte.astype(np.uint8).reshape(k // 512, 16, n))


def unpack_weight(words, scales, fmt):
    g, _, n = scales.shape
    words = np.ascontiguousarray(words).reshape(g, 128, n, -1)
    if fmt == "e4m3":
        vals = words.view(ml_dtypes.float8_e4m3fn).astype(np.float64)
    else:
        nib = np.empty((g, 128, n, 4), np.uint8)
        nib[..., 0::2] = words & 0xF
        nib[..., 1::2] = words >> 4
        vals = E2M1[nib]
    vals = vals * np.repeat(np.exp2(scales.astype(np.float64) - 127.0), 8, axis=1)[..., None]
    return vals.transpose(0, 1, 3, 2).reshape(g * 512, n)


def gelu(v):
    return 0.5 * v * (1.0 + np.tanh(np.sqrt(2.0 / np.pi) * (v + 0.044715 * v**3)))


def often(T, S):
    return np.random.permutation(T)[(T * np.random.uniform(0, 1, S) ** 4).astype(np.int64)]


T, T2, S, K, K2, H, N = 2048, 1024, 512, 1024, 512, 1024, 256

def setup_inputs():
    n = np.random.standard_normal
    s = mx_kscale(K)[:, None]
    s2 = mx_kscale(K2)[:, None]
    u = mx_kscale(H)[:, None]
    tab_words, tab_scales = pack_weight(n((K, T)) * s, "e4m3")
    tab2_words, tab2_scales = pack_weight(n((K2, T2)) * s2, "e2m1")
    w1_words, w1_scales = pack_weight(n((K, H)) / np.sqrt(K) / s, "e2m1")
    w3_words, w3_scales = pack_weight(n((K2, H)) / np.sqrt(K2) / s2, "e4m3")
    return {
        "tab_words": tab_words, "tab_scales": tab_scales,
        "tab2_words": tab2_words, "tab2_scales": tab2_scales,
        "offs": striped(often(T, S)),
        "offs2": striped(often(T2, S)),
        "w1_words": w1_words, "w1_scales": w1_scales,
        "w2": (n((K2, H)) / np.sqrt(K2) / s2).astype(np.float32),
        "w3_words": w3_words, "w3_scales": w3_scales,
        "gain": (np.exp(0.3 * n(H)) * u[:, 0]).astype(np.float32),
        "w4": (1.5 * n((H, N)) / np.sqrt(H) / u).astype(np.float32),
    }

def reference(tab_words, tab_scales, tab2_words, tab2_scales, offs, offs2,
              w1_words, w1_scales, w2, w3_words, w3_scales, gain, w4):
    v = unpack_weight(tab_words, tab_scales, "e4m3")[:, unstriped(offs)]
    v2 = unpack_weight(tab2_words, tab2_scales, "e2m1")[:, unstriped(offs2)]
    motion = unpack_weight(w1_words, w1_scales, "e2m1").T @ v
    scale = mxq(f64(w2), 0, "e4m3").T @ v2
    shift = unpack_weight(w3_words, w3_scales, "e4m3").T @ v2
    x = motion * (1.0 + np.tanh(scale)) + shift
    h = f64(gain)[:, None] * (x / (1.0 + np.exp(-x)))
    return mxq(f64(w4), 0, "e4m3").T @ mxq(h, 0, "e4m3")

@@ -1,0 +1,265 @@
+from contextlib import ExitStack
+
+import concourse.mybir as mybir
+from concourse.masks import make_identity
+
+T, T2, S, K, K2, H, N = 2048, 1024, 512, 1024, 512, 1024, 256
+FLOPS = 2 * S * (K * H + 2 * K2 * H + H * N)
+
+F32 = mybir.dt.float32
+BF16 = mybir.dt.bfloat16
+I32 = mybir.dt.int32
+U32 = mybir.dt.uint32
+U16 = mybir.dt.uint16
+U8 = mybir.dt.uint8
+FP8X4 = mybir.dt.float8_e4m3fn_x4
+FP4X4 = mybir.dt.float4_e2m1fn_x4
+ACT = mybir.ActivationFunctionType
+ALU = mybir.AluOpType
+
+P = 128
+PACK = 4
+KP = P * PACK
+JC = 128
+CHUNKS = S // JC
+HALVES = H // KP
+
+
+def tile_list_gait_breed_grading_kernel(tc, tab_words, tab_scales, tab2_words, tab2_scales, offs, offs2,
+                                                 w1_words, w1_scales, w2, w3_words, w3_scales, gain, w4, out):
+    nc = tc.nc
+    with ExitStack() as ctx:
+        keep = ctx.enter_context(tc.tile_pool(name="keep", bufs=1))
+        ring = ctx.enter_context(tc.tile_pool(name="ring", bufs=3))
+        psum = ctx.enter_context(tc.psum_pool(name="psum", bufs=2))
+
+        def held(shape, dtype, name):
+            return keep.tile(shape, dtype, name=name, align_bytes=64)
+
+        list1 = held([P, S // 16], U16, "list1")
+        list2 = held([P, S // 16], U16, "list2")
+        tab2w = held([P, T2], U16, "tab2w")
+        tab2s = held([P, T2], U8, "tab2s")
+        tabw = [held([P, T], U32, f"tabw{a}") for a in range(2)]
+        tabs = held([P, T], U8, "tabs")
+        wsraw = held([P, 3, H], U8, "wsraw")
+        v1s = held([P, S], U8, "v1s")
+        warm = held([P, 2], F32, "warm")
+
+        nc.vector.memset(warm[:, 0:1], 0.0)
+        nc.scalar.activation(out=warm[:, 1:2], in_=warm[:, 0:1], func=ACT.Silu)
+        nc.vector.memset(tab2s[:].bitcast(I32), 0)
+        nc.vector.memset(tabs[:].bitcast(I32), 0)
+        nc.gpsimd.memset(wsraw[:].rearrange("p a n -> p (a n)").bitcast(I32), 0)
+        nc.vector.memset(v1s[:].bitcast(I32), 0)
+
+        w2raw = [[held([P, PACK, KP // 2], F32, f"w2raw{b}{q}") for q in range(2)] for b in range(HALVES)]
+        w1raw = [held([P, 2, KP // 2], I32, f"w1raw{b}") for b in range(HALVES)]
+        w3raw = [held([P, KP], I32, f"w3raw{b}") for b in range(HALVES)]
+        w4raw = [held([P, PACK, N], F32, f"w4raw{b}") for b in range(HALVES)]
+        gains = held([P, HALVES, PACK], F32, "gains")
+        grows = held([P, P], F32, "grows")
+        ident = held([P, P], F32, "ident")
+        nc.vector.memset(grows[:], 0.0)
+
+        def load_w2(b):
+            for q in range(2):
+                c0 = b * KP + q * KP // 2
+                nc.sync.dma_start(out=w2raw[b][q][:], in_=w2[:, c0:c0 + KP // 2].rearrange("(p j) c -> p j c", j=PACK))
+
+        def load_w13(b):
+            nc.sync.dma_start(out=w3raw[b][:],
+                              in_=w3_words[0].rearrange("p n t -> p (n t)")[:, 4 * KP * b:4 * KP * (b + 1)].bitcast(I32))
+            nc.sync.dma_start(out=w1raw[b][:],
+                              in_=w1_words.rearrange("a p n -> p a n")[:, :, 2 * KP * b:2 * KP * (b + 1)].bitcast(I32))
+
+        nc.sync.dma_start(list2[:], offs2)
+        nc.sync.dma_start(out=tab2w[:].bitcast(I32), in_=tab2_words[0].bitcast(I32))
+        for q in range(4):
+            nc.sync.dma_start(out=tab2s[32 * q:32 * q + 4, :].bitcast(I32), in_=tab2_scales[0, 4 * q:4 * q + 4, :].bitcast(I32))
+        load_w2(0)
+        nc.sync.dma_start(list1[:], offs)
+        for q in range(4):
+            nc.sync.dma_start(out=tabs[32 * q:32 * q + 8, :].bitcast(I32), in_=tab_scales[:, 4 * q:4 * q + 4, :].bitcast(I32))
+        for q in range(4):
+            nc.gpsimd.dma_start(out=wsraw[32 * q:32 * q + 4, 0:2, :].bitcast(I32),
+                                in_=w1_scales[:, 4 * q:4 * q + 4, :].rearrange("a r n -> r a n").bitcast(I32))
+        load_w13(0)
+        nc.sync.dma_start(out=tabw[0][:].bitcast(I32), in_=tab_words[0].rearrange("p n t -> p (n t)").bitcast(I32))
+        for q in range(4):
+            nc.sync.dma_start(out=wsraw[32 * q:32 * q + 4, 2, :].bitcast(I32),
+                              in_=w3_scales[0, 4 * q:4 * q + 4, :].bitcast(I32))
+        nc.sync.dma_start(out=tabw[1][:].bitcast(I32), in_=tab_words[1].rearrange("p n t -> p (n t)").bitcast(I32))
+        for b in range(HALVES):
+            nc.sync.dma_start(out=grows[PACK * b:PACK * (b + 1), :].rearrange("t (g i) -> t g i", i=8),
+                              in_=gain[b * KP:(b + 1) * KP].rearrange("(g t i) -> t g i", t=PACK, i=8))
+        make_identity(nc, ident[:])
+        load_w2(1)
+        load_w13(1)
+        for b in range(HALVES):
+            rows = w4[b * KP:(b + 1) * KP, :].rearrange("(g t i) n -> t g i n", t=PACK, i=8)
+            for t in range(PACK):
+                nc.sync.dma_start(out=w4raw[b][:, t, :], in_=rows[t])
+
+        v2w = held([P, S], U16, "v2w")
+        v2s = held([P, S], U8, "v2s")
+        nc.vector.tensor_copy(out=v2w[:], in_=tab2w[:].indirect(list2[:]))
+        nc.vector.tensor_copy(out=v2s[:], in_=tab2s[:].indirect(list2[:]))
+        v0s = held([P, S], U8, "v0s")
+        nc.vector.tensor_copy(out=v0s[:], in_=tabs[:].indirect(list1[:]))
+        nc.scalar.dma_start(out=v1s[0:100, :].bitcast(I32), in_=v0s[4:104, :].bitcast(I32))
+        vs = [v0s, v1s]
+
+        w2g = [held([P, KP * PACK], BF16, f"w2g{b}") for b in range(HALVES)]
+        w2c = [held([P, KP], U32, f"w2c{b}") for b in range(HALVES)]
+        w2s = [held([P, KP], U8, f"w2s{b}") for b in range(HALVES)]
+
+        def prepare_w2(b):
+            dst = w2g[b][:].rearrange("p (t q g i j) -> p q t g i j", t=PACK, q=2, i=8, j=PACK)
+            for q in range(2):
+                nc.scalar.copy(out=dst[:, q], in_=w2raw[b][q][:].rearrange("p j (g t i) -> p t g i j", t=PACK, i=8))
+            nc.vector.quantize_mx(out=w2c[b][:].bitcast(FP8X4), scales=w2s[b][:], in_=w2g[b][:])
+
+        ws = held([P, 3 * H // 4], I32, "ws")
+        w1c = [held([P, 2, KP // 2], I32, f"w1c{b}") for b in range(HALVES)]
+        w3c = [held([P, KP], I32, f"w3c{b}") for b in range(HALVES)]
+
+        def order_scales():
+            nc.vector.tensor_copy(
+                out=ws[:].rearrange("p (a t g w) -> p a t g w", t=PACK, g=16, w=2),
+                in_=wsraw[:].rearrange("p a n -> p (a n)").bitcast(I32).rearrange("p (a g t w) -> p a t g w", t=PACK, g=16, w=2))
+
+        def order_w13(b):
+            nc.vector.tensor_copy(out=w3c[b][:].rearrange("p (t g w) -> p t g w", t=PACK, w=8),
+                                  in_=w3raw[b][:].rearrange("p (g t w) -> p t g w", t=PACK, w=8))
+            nc.vector.tensor_copy(out=w1c[b][:].rearrange("p a (t g w) -> p a t g w", t=PACK, w=4),
+                                  in_=w1raw[b][:].rearrange("p a (g t w) -> p a t g w", t=PACK, w=4))
+
+        def wscale(a, b, t):
+            c0 = (a * H + b * KP + t * P) // 4
+            return ws[:, c0:c0 + P // 4].bitcast(U8)
+
+        vw = [[held([P, S // 2], U32, f"vw{a}{q}") for q in range(2)] for a in range(2)]
+
+        def gather_words(a, q):
+            nc.vector.tensor_copy(out=vw[a][q][:], in_=tabw[a][:].indirect(list1[:, 16 * q:16 * (q + 1)]))
+
+        units = [(b, c) for b in range(HALVES) for c in range(CHUNKS)]
+        th, aa, ss, hb = {}, {}, {}, {}
+        groups = [(0, 4), (4, 6), (6, 7), (7, 8)]
+        hc, hs, hg = {}, {}, {}
+        for lo, hi in groups:
+            codes = held([P, (hi - lo) * JC], U32, f"hc{lo}")
+            plane = held([P, (hi - lo) * JC], U8, f"hs{lo}")
+            wide = held([P, (hi - lo) * JC, PACK], BF16, f"hb{lo}")
+            hg[hi - 1] = (codes, plane, wide)
+            for u in range(lo, hi):
+                hc[u] = codes[:, (u - lo) * JC:(u - lo + 1) * JC]
+                hs[u] = plane[:, (u - lo) * JC:(u - lo + 1) * JC]
+                hb[u] = wide[:, (u - lo) * JC:(u - lo + 1) * JC, :]
+
+        def cols(c):
+            return slice(c * JC, (c + 1) * JC)
+
+        def woven(bank):
+            return bank[:].rearrange("p t j -> p j t")
+
+        def do_tanh(u):
+            b, c = units[u]
+            bank = psum.tile([P, PACK, JC], F32, name="sc")
+            for t in range(PACK):
+                nc.tensor.matmul_mx(out=bank[:, t, :], lhsT=w2c[b][:, t * P:(t + 1) * P].bitcast(FP8X4),
+                                    lhsT_scale=w2s[b][:, t * P:(t + 1) * P],
+                                    rhs=v2w[:, cols(c)].bitcast(FP4X4), rhs_scale=v2s[:, cols(c)], start=True, stop=True)
+            th[u] = ring.tile([P, JC, PACK], F32, name="th", bufs=5)
+            nc.scalar.activation(out=th[u][:], in_=woven(bank), func=ACT.Tanh)
+
+        def do_mul(u):
+            b, c = units[u]
+            bank = psum.tile([P, PACK, JC], F32, name="mo")
+            for t in range(PACK):
+                for a in range(2):
+                    nc.tensor.matmul_mx(out=bank[:, t, :],
+                                        lhsT=w1c[b][:, a, t * P // 2:(t + 1) * P // 2].bitcast(FP4X4),
+                                        lhsT_scale=wscale(a, b, t),
+                                        rhs=vw[a][c // 2][:, cols(c % 2)].bitcast(FP8X4), rhs_scale=vs[a][:, cols(c)],
+                                        start=(a == 0), stop=(a == 1))
+            aa[u] = ring.tile([P, JC, PACK], F32, name="aa")
+            nc.vector.scalar_tensor_tensor(out=aa[u][:], in0=th[u][:], scalar=1.0, in1=woven(bank), op0=ALU.add, op1=ALU.mult)
+
+        def do_add(u):
+            b, c = units[u]
+            bank = psum.tile([P, PACK, JC], F32, name="sh")
+            for t in range(PACK):
+                nc.tensor.matmul_mx(out=bank[:, t, :], lhsT=w3c[b][:, t * P:(t + 1) * P].bitcast(FP8X4),
+                                    lhsT_scale=wscale(2, b, t),
+                                    rhs=v2w[:, cols(c)].bitcast(FP4X4), rhs_scale=v2s[:, cols(c)], start=True, stop=True)
+            xx = ring.tile([P, JC, PACK], F32, name="xx")
+            nc.vector.tensor_tensor(out=xx[:], in0=woven(bank), in1=aa[u][:], op=ALU.add)
+            ss[u] = ring.tile([P, JC, PACK], F32, name="ss")
+            nc.scalar.activation(out=ss[u][:], in_=xx[:], func=ACT.Silu)
+
+        def do_gain(u):
+            b, c = units[u]
+            nc.vector.tensor_tensor(out=hb[u], in0=ss[u][:], in1=gains[:, b, :].unsqueeze(1).to_broadcast([P, JC, PACK]),
+                                    op=ALU.mult)
+
+        def do_quant(u):
+            codes, plane, wide = hg[u]
+            nc.vector.quantize_mx(out=codes[:].bitcast(FP8X4), scales=plane[:], in_=wide[:].rearrange("p j t -> p (j t)"))
+
+        w4g = held([P, HALVES, N, PACK], BF16, "w4g")
+        w4c = held([P, HALVES * N], U32, "w4c")
+        w4s = held([P, HALVES * N], U8, "w4s")
+
+        def prepare_w4():
+            for b in range(HALVES):
+                nc.scalar.copy(out=w4g[:, b], in_=w4raw[b][:].rearrange("p t n -> p n t"))
+            nc.vector.quantize_mx(out=w4c[:].bitcast(FP8X4), scales=w4s[:], in_=w4g[:].rearrange("p b n t -> p (b n t)"))
+
+        def do_out(c):
+            bank = psum.tile([P, N // P, JC], F32, name="ob")
+            for h in range(N // P):
+                for b in range(HALVES):
+                    u = b * CHUNKS + c
+                    w = slice(b * N + h * P, b * N + (h + 1) * P)
+                    nc.tensor.matmul_mx(out=bank[:, h, :], lhsT=w4c[:, w].bitcast(FP8X4), lhsT_scale=w4s[:, w],
+                                        rhs=hc[u].bitcast(FP8X4), rhs_scale=hs[u], start=(b == 0), stop=(b == HALVES - 1))
+            res = ring.tile([P, N // P, JC], F32, name="res", bufs=4)
+            nc.scalar.copy(out=res[:], in_=bank[:])
+            nc.sync.dma_start(out=out.rearrange("(h p) j -> p h j", p=P)[:, :, cols(c)], in_=res[:])
+
+        prepare_w2(0)
+        for u in range(CHUNKS):
+            do_tanh(u)
+        turned = psum.tile([P, P], F32, name="ob")
+        nc.tensor.transpose(turned[:], grows[:], ident[:])
+        nc.scalar.copy(out=gains[:].rearrange("p b t -> p (b t)"), in_=turned[:, 0:HALVES * PACK])
+        order_scales()
+        order_w13(0)
+        gather_words(0, 0)
+        gather_words(0, 1)
+        gather_words(1, 0)
+        n = len(units)
+        for s in range(n + 3):
+            if s < n:
+                do_mul(s)
+            if s == 0:
+                gather_words(1, 1)
+            if s == 1:
+                prepare_w2(1)
+                order_w13(1)
+            if 2 <= s < 2 + CHUNKS:
+                do_tanh(s + 2)
+            if s == 5:
+                prepare_w4()
+            if 0 <= s - 1 < n:
+                do_add(s - 1)
+            if 0 <= s - 2 < n:
+                do_gain(s - 2)
+            if s - 3 in hg:
+                do_quant(s - 3)
+                for lo, hi in groups:
+                    if hi - 1 == s - 3 and lo >= CHUNKS:
+                        for u in range(lo, hi):
+                            do_out(u - CHUNKS)

@@ -33,25 +33,25 @@ def tile_list_gait_breed_grading_kernel(tc, tab_words, tab_scales, tab2_words, t
         ring = ctx.enter_context(tc.tile_pool(name="ring", bufs=3))
         psum = ctx.enter_context(tc.psum_pool(name="psum", bufs=2))
 
-        def held(shape, dtype, name):
-            return keep.tile(shape, dtype, name=name, align_bytes=64)
+        def held(shape, dtype, name, tag=None):
+            return keep.tile(shape, dtype, name=name, tag=tag or name, align_bytes=64)
 
         list1 = held([P, S // 16], U16, "list1")
         list2 = held([P, S // 16], U16, "list2")
         tab2w = held([P, T2], U16, "tab2w")
         tab2s = held([P, T2], U8, "tab2s")
         tabw = [held([P, T], U32, f"tabw{a}") for a in range(2)]
-        tabs = held([P, T], U8, "tabs")
-        wsraw = held([P, 3, H], U8, "wsraw")
-        v1s = held([P, S], U8, "v1s")
+        tabs = held([P, 2, T], U8, "tabs")
+        w1sraw = held([P, 2, H], U8, "w1sraw")
+        w3sraw = held([P, H], U8, "w3sraw")
         warm = held([P, 2], F32, "warm")
 
         nc.vector.memset(warm[:, 0:1], 0.0)
         nc.scalar.activation(out=warm[:, 1:2], in_=warm[:, 0:1], func=ACT.Silu)
+        nc.gpsimd.memset(w3sraw[:].bitcast(I32), 0)
         nc.vector.memset(tab2s[:].bitcast(I32), 0)
-        nc.vector.memset(tabs[:].bitcast(I32), 0)
-        nc.gpsimd.memset(wsraw[:].rearrange("p a n -> p (a n)").bitcast(I32), 0)
-        nc.vector.memset(v1s[:].bitcast(I32), 0)
+        nc.vector.memset(tabs[:].rearrange("p a n -> p (a n)").bitcast(I32), 0)
+        nc.gpsimd.memset(w1sraw[:].rearrange("p a n -> p (a n)").bitcast(I32), 0)
 
         w2raw = [[held([P, PACK, KP // 2], F32, f"w2raw{b}{q}") for q in range(2)] for b in range(HALVES)]
         w1raw = [held([P, 2, KP // 2], I32, f"w1raw{b}") for b in range(HALVES)]
@@ -62,14 +62,15 @@ def tile_list_gait_breed_grading_kernel(tc, tab_words, tab_scales, tab2_words, t
         ident = held([P, P], F32, "ident")
         nc.vector.memset(grows[:], 0.0)
 
-        def load_w2(b):
-            for q in range(2):
-                c0 = b * KP + q * KP // 2
-                nc.sync.dma_start(out=w2raw[b][q][:], in_=w2[:, c0:c0 + KP // 2].rearrange("(p j) c -> p j c", j=PACK))
+        def load_w2(b, q):
+            c0 = b * KP + q * KP // 2
+            nc.sync.dma_start(out=w2raw[b][q][:], in_=w2[:, c0:c0 + KP // 2].rearrange("(p j) c -> p j c", j=PACK))
 
-        def load_w13(b):
+        def load_w3(b):
             nc.sync.dma_start(out=w3raw[b][:],
                               in_=w3_words[0].rearrange("p n t -> p (n t)")[:, 4 * KP * b:4 * KP * (b + 1)].bitcast(I32))
+
+        def load_w1(b):
             nc.sync.dma_start(out=w1raw[b][:],
                               in_=w1_words.rearrange("a p n -> p a n")[:, :, 2 * KP * b:2 * KP * (b + 1)].bitcast(I32))
 
@@ -77,25 +78,30 @@ def tile_list_gait_breed_grading_kernel(tc, tab_words, tab_scales, tab2_words, t
         nc.sync.dma_start(out=tab2w[:].bitcast(I32), in_=tab2_words[0].bitcast(I32))
         for q in range(4):
             nc.sync.dma_start(out=tab2s[32 * q:32 * q + 4, :].bitcast(I32), in_=tab2_scales[0, 4 * q:4 * q + 4, :].bitcast(I32))
-        load_w2(0)
         nc.sync.dma_start(list1[:], offs)
+        load_w2(0, 0)
         for q in range(4):
-            nc.sync.dma_start(out=tabs[32 * q:32 * q + 8, :].bitcast(I32), in_=tab_scales[:, 4 * q:4 * q + 4, :].bitcast(I32))
-        for q in range(4):
-            nc.gpsimd.dma_start(out=wsraw[32 * q:32 * q + 4, 0:2, :].bitcast(I32),
-                                in_=w1_scales[:, 4 * q:4 * q + 4, :].rearrange("a r n -> r a n").bitcast(I32))
-        load_w13(0)
+            nc.sync.dma_start(out=tabs[32 * q:32 * q + 4].bitcast(I32),
+                              in_=tab_scales[:, 4 * q:4 * q + 4, :].rearrange("a r n -> r a n").bitcast(I32))
+        load_w2(0, 1)
         nc.sync.dma_start(out=tabw[0][:].bitcast(I32), in_=tab_words[0].rearrange("p n t -> p (n t)").bitcast(I32))
         for q in range(4):
-            nc.sync.dma_start(out=wsraw[32 * q:32 * q + 4, 2, :].bitcast(I32),
-                              in_=w3_scales[0, 4 * q:4 * q + 4, :].bitcast(I32))
+            nc.sync.dma_start(out=w1sraw[32 * q:32 * q + 4].bitcast(I32),
+                              in_=w1_scales[:, 4 * q:4 * q + 4, :].rearrange("a r n -> r a n").bitcast(I32))
+        load_w1(0)
         nc.sync.dma_start(out=tabw[1][:].bitcast(I32), in_=tab_words[1].rearrange("p n t -> p (n t)").bitcast(I32))
+        load_w3(0)
+        for q in range(4):
+            nc.sync.dma_start(out=w3sraw[32 * q:32 * q + 4, :].bitcast(I32),
+                              in_=w3_scales[0, 4 * q:4 * q + 4, :].bitcast(I32))
+        load_w2(1, 0)
+        load_w2(1, 1)
         for b in range(HALVES):
             nc.sync.dma_start(out=grows[PACK * b:PACK * (b + 1), :].rearrange("t (g i) -> t g i", i=8),
                               in_=gain[b * KP:(b + 1) * KP].rearrange("(g t i) -> t g i", t=PACK, i=8))
+        load_w1(1)
+        load_w3(1)
         make_identity(nc, ident[:])
-        load_w2(1)
-        load_w13(1)
         for b in range(HALVES):
             rows = w4[b * KP:(b + 1) * KP, :].rearrange("(g t i) n -> t g i n", t=PACK, i=8)
             for t in range(PACK):
@@ -105,39 +111,45 @@ def tile_list_gait_breed_grading_kernel(tc, tab_words, tab_scales, tab2_words, t
         v2s = held([P, S], U8, "v2s")
         nc.vector.tensor_copy(out=v2w[:], in_=tab2w[:].indirect(list2[:]))
         nc.vector.tensor_copy(out=v2s[:], in_=tab2s[:].indirect(list2[:]))
-        v0s = held([P, S], U8, "v0s")
-        nc.vector.tensor_copy(out=v0s[:], in_=tabs[:].indirect(list1[:]))
-        nc.scalar.dma_start(out=v1s[0:100, :].bitcast(I32), in_=v0s[4:104, :].bitcast(I32))
-        vs = [v0s, v1s]
+        vs = [held([P, S], U8, f"vs{a}") for a in range(2)]
+        for a in range(2):
+            nc.vector.tensor_copy(out=vs[a][:], in_=tabs[:, a, :].indirect(list1[:]))
 
-        w2g = [held([P, KP * PACK], BF16, f"w2g{b}") for b in range(HALVES)]
-        w2c = [held([P, KP], U32, f"w2c{b}") for b in range(HALVES)]
+        w2g, w2c = {}, {}
         w2s = [held([P, KP], U8, f"w2s{b}") for b in range(HALVES)]
 
-        def prepare_w2(b):
+        def round_w2(b, rounded_tag):
+            w2g[b] = held([P, KP * PACK], BF16, f"w2g{b}", rounded_tag)
             dst = w2g[b][:].rearrange("p (t q g i j) -> p q t g i j", t=PACK, q=2, i=8, j=PACK)
             for q in range(2):
                 nc.scalar.copy(out=dst[:, q], in_=w2raw[b][q][:].rearrange("p j (g t i) -> p t g i j", t=PACK, i=8))
+
+        def quantise_w2(b, codes_tag):
+            w2c[b] = held([P, KP], U32, f"w2c{b}", codes_tag)
             nc.vector.quantize_mx(out=w2c[b][:].bitcast(FP8X4), scales=w2s[b][:], in_=w2g[b][:])
 
-        ws = held([P, 3 * H // 4], I32, "ws")
-        w1c = [held([P, 2, KP // 2], I32, f"w1c{b}") for b in range(HALVES)]
-        w3c = [held([P, KP], I32, f"w3c{b}") for b in range(HALVES)]
+        w1s = held([P, 2 * H // 4], I32, "w1s")
+        w3s = held([P, H // 4], I32, "w3s")
+        w1c, w3c = {}, {}
 
-        def order_scales():
-            nc.vector.tensor_copy(
-                out=ws[:].rearrange("p (a t g w) -> p a t g w", t=PACK, g=16, w=2),
-                in_=wsraw[:].rearrange("p a n -> p (a n)").bitcast(I32).rearrange("p (a g t w) -> p a t g w", t=PACK, g=16, w=2))
+        def order_scales(dst, raw):
+            nc.vector.tensor_copy(out=dst[:].rearrange("p (a t g w) -> p a t g w", t=PACK, g=16, w=2),
+                                  in_=raw.bitcast(I32).rearrange("p (a g t w) -> p a t g w", t=PACK, g=16, w=2))
 
-        def order_w13(b):
-            nc.vector.tensor_copy(out=w3c[b][:].rearrange("p (t g w) -> p t g w", t=PACK, w=8),
+        def order_w3(b, tag):
+            w3c[b] = held([P, KP], I32, f"w3c{b}", tag)
+            nc.gpsimd.tensor_copy(out=w3c[b][:].rearrange("p (t g w) -> p t g w", t=PACK, w=8),
                                   in_=w3raw[b][:].rearrange("p (g t w) -> p t g w", t=PACK, w=8))
-            nc.vector.tensor_copy(out=w1c[b][:].rearrange("p a (t g w) -> p a t g w", t=PACK, w=4),
-                                  in_=w1raw[b][:].rearrange("p a (g t w) -> p a t g w", t=PACK, w=4))
 
-        def wscale(a, b, t):
+        def order_w1(b, tag):
+            w1c[b] = held([P, 2, KP // 2], I32, f"w1c{b}", tag)
+            for a in range(2):
+                nc.gpsimd.tensor_copy(out=w1c[b][:, a, :].rearrange("p (t g w) -> p t g w", t=PACK, w=4),
+                                      in_=w1raw[b][:, a, :].rearrange("p (g t w) -> p t g w", t=PACK, w=4))
+
+        def wscale(plane, a, b, t):
             c0 = (a * H + b * KP + t * P) // 4
-            return ws[:, c0:c0 + P // 4].bitcast(U8)
+            return plane[:, c0:c0 + P // 4].bitcast(U8)
 
         vw = [[held([P, S // 2], U32, f"vw{a}{q}") for q in range(2)] for a in range(2)]
 
@@ -146,6 +158,8 @@ def tile_list_gait_breed_grading_kernel(tc, tab_words, tab_scales, tab2_words, t
 
         units = [(b, c) for b in range(HALVES) for c in range(CHUNKS)]
         th, aa, ss, hb = {}, {}, {}, {}
+        reuse = {"ss0": "w2raw10", "ss1": "w2raw11", "ss5": "w4raw0", "ss6": "w4raw1", "aa3": "w2c0",
+                 "xx7": "w2c0"}
         groups = [(0, 4), (4, 6), (6, 7), (7, 8)]
         hc, hs, hg = {}, {}, {}
         for lo, hi in groups:
@@ -171,20 +185,20 @@ def tile_list_gait_breed_grading_kernel(tc, tab_words, tab_scales, tab2_words, t
                 nc.tensor.matmul_mx(out=bank[:, t, :], lhsT=w2c[b][:, t * P:(t + 1) * P].bitcast(FP8X4),
                                     lhsT_scale=w2s[b][:, t * P:(t + 1) * P],
                                     rhs=v2w[:, cols(c)].bitcast(FP4X4), rhs_scale=v2s[:, cols(c)], start=True, stop=True)
-            th[u] = ring.tile([P, JC, PACK], F32, name="th", bufs=5)
+            th[u] = held([P, JC, PACK], F32, f"th{u}")
             nc.scalar.activation(out=th[u][:], in_=woven(bank), func=ACT.Tanh)
 
         def do_mul(u):
             b, c = units[u]
             bank = psum.tile([P, PACK, JC], F32, name="mo")
-            for t in range(PACK):
-                for a in range(2):
+            for a in range(2):
+                for t in range(PACK):
                     nc.tensor.matmul_mx(out=bank[:, t, :],
                                         lhsT=w1c[b][:, a, t * P // 2:(t + 1) * P // 2].bitcast(FP4X4),
-                                        lhsT_scale=wscale(a, b, t),
+                                        lhsT_scale=wscale(w1s, a, b, t),
                                         rhs=vw[a][c // 2][:, cols(c % 2)].bitcast(FP8X4), rhs_scale=vs[a][:, cols(c)],
-                                        start=(a == 0), stop=(a == 1))
-            aa[u] = ring.tile([P, JC, PACK], F32, name="aa")
+                                        start=(a == 0 and t == 0), stop=(a == 1 and t == PACK - 1))
+            aa[u] = held([P, JC, PACK], F32, f"aa{u}", reuse.get(f"aa{u}"))
             nc.vector.scalar_tensor_tensor(out=aa[u][:], in0=th[u][:], scalar=1.0, in1=woven(bank), op0=ALU.add, op1=ALU.mult)
 
         def do_add(u):
@@ -192,69 +206,86 @@ def tile_list_gait_breed_grading_kernel(tc, tab_words, tab_scales, tab2_words, t
             bank = psum.tile([P, PACK, JC], F32, name="sh")
             for t in range(PACK):
                 nc.tensor.matmul_mx(out=bank[:, t, :], lhsT=w3c[b][:, t * P:(t + 1) * P].bitcast(FP8X4),
-                                    lhsT_scale=wscale(2, b, t),
+                                    lhsT_scale=wscale(w3s, 0, b, t),
                                     rhs=v2w[:, cols(c)].bitcast(FP4X4), rhs_scale=v2s[:, cols(c)], start=True, stop=True)
-            xx = ring.tile([P, JC, PACK], F32, name="xx")
+            xx = held([P, JC, PACK], F32, f"xx{u}", reuse.get(f"xx{u}"))
             nc.vector.tensor_tensor(out=xx[:], in0=woven(bank), in1=aa[u][:], op=ALU.add)
-            ss[u] = ring.tile([P, JC, PACK], F32, name="ss")
+            ss[u] = held([P, JC, PACK], F32, f"ss{u}", reuse.get(f"ss{u}"))
             nc.scalar.activation(out=ss[u][:], in_=xx[:], func=ACT.Silu)
 
         def do_gain(u):
             b, c = units[u]
-            nc.vector.tensor_tensor(out=hb[u], in0=ss[u][:], in1=gains[:, b, :].unsqueeze(1).to_broadcast([P, JC, PACK]),
+            eng = nc.gpsimd if u < 6 else nc.vector
+            eng.tensor_tensor(out=hb[u], in0=ss[u][:], in1=gains[:, b, :].unsqueeze(1).to_broadcast([P, JC, PACK]),
                                     op=ALU.mult)
 
         def do_quant(u):
             codes, plane, wide = hg[u]
             nc.vector.quantize_mx(out=codes[:].bitcast(FP8X4), scales=plane[:], in_=wide[:].rearrange("p j t -> p (j t)"))
 
-        w4g = held([P, HALVES, N, PACK], BF16, "w4g")
-        w4c = held([P, HALVES * N], U32, "w4c")
         w4s = held([P, HALVES * N], U8, "w4s")
+        w4q = {}
 
-        def prepare_w4():
+        def round_w4():
+            w4g = held([P, HALVES, N, PACK], BF16, "w4g", "w2c0")
+            w4q[1] = w4g
             for b in range(HALVES):
                 nc.scalar.copy(out=w4g[:, b], in_=w4raw[b][:].rearrange("p t n -> p n t"))
+
+        def quantise_w4():
+            w4g = w4q[1]
+            w4c = held([P, HALVES * N], U32, "w4c", "th5")
+            w4q[0] = w4c
             nc.vector.quantize_mx(out=w4c[:].bitcast(FP8X4), scales=w4s[:], in_=w4g[:].rearrange("p b n t -> p (b n t)"))
 
         def do_out(c):
             bank = psum.tile([P, N // P, JC], F32, name="ob")
-            for h in range(N // P):
-                for b in range(HALVES):
+            for b in range(HALVES):
+                for h in range(N // P):
                     u = b * CHUNKS + c
                     w = slice(b * N + h * P, b * N + (h + 1) * P)
-                    nc.tensor.matmul_mx(out=bank[:, h, :], lhsT=w4c[:, w].bitcast(FP8X4), lhsT_scale=w4s[:, w],
-                                        rhs=hc[u].bitcast(FP8X4), rhs_scale=hs[u], start=(b == 0), stop=(b == HALVES - 1))
+                    nc.tensor.matmul_mx(out=bank[:, h, :], lhsT=w4q[0][:, w].bitcast(FP8X4), lhsT_scale=w4s[:, w],
+                                        rhs=hc[u].bitcast(FP8X4), rhs_scale=hs[u], start=(b == 0 and h == 0),
+                                        stop=(b == HALVES - 1 and h == N // P - 1))
             res = ring.tile([P, N // P, JC], F32, name="res", bufs=4)
             nc.scalar.copy(out=res[:], in_=bank[:])
             nc.sync.dma_start(out=out.rearrange("(h p) j -> p h j", p=P)[:, :, cols(c)], in_=res[:])
 
-        prepare_w2(0)
+        round_w2(0, "w2g0")
+        quantise_w2(0, "w2c0")
         for u in range(CHUNKS):
             do_tanh(u)
-        turned = psum.tile([P, P], F32, name="ob")
-        nc.tensor.transpose(turned[:], grows[:], ident[:])
-        nc.scalar.copy(out=gains[:].rearrange("p b t -> p (b t)"), in_=turned[:, 0:HALVES * PACK])
-        order_scales()
-        order_w13(0)
         gather_words(0, 0)
         gather_words(0, 1)
+        order_scales(w1s, w1sraw[:].rearrange("p a n -> p (a n)"))
+        order_w1(0, "w1c0")
         gather_words(1, 0)
+        order_w3(0, "w3c0")
+        order_scales(w3s, w3sraw[:])
         n = len(units)
+        round_w2(1, "w2c0")
         for s in range(n + 3):
+            if s == 3:
+                quantise_w2(1, "th2")
+                order_w3(1, "w3c1")
+            if 3 <= s < 3 + CHUNKS:
+                do_tanh(s + 1)
             if s < n:
                 do_mul(s)
             if s == 0:
                 gather_words(1, 1)
             if s == 1:
-                prepare_w2(1)
-                order_w13(1)
-            if 2 <= s < 2 + CHUNKS:
-                do_tanh(s + 2)
-            if s == 5:
-                prepare_w4()
+                order_w1(1, "w1c1")
+            if s == 6:
+                quantise_w4()
             if 0 <= s - 1 < n:
                 do_add(s - 1)
+            if s == 4:
+                round_w4()
+            if s == 1:
+                turned = psum.tile([P, P], F32, name="sh")
+                nc.tensor.transpose(turned[:], grows[:], ident[:])
+                nc.scalar.copy(out=gains[:].rearrange("p b t -> p (b t)"), in_=turned[:, 0:HALVES * PACK])
             if 0 <= s - 2 < n:
                 do_gain(s - 2)
             if s - 3 in hg:

@@ -159,21 +159,15 @@ def tile_list_gait_breed_grading_kernel(tc, tab_words, tab_scales, tab2_words, t
         units = [(b, c) for b in range(HALVES) for c in range(CHUNKS)]
         th, aa, ss, hb = {}, {}, {}, {}
         reuse = {"ss0": "w2raw10", "ss1": "w2raw11", "ss5": "w4raw0", "ss6": "w4raw1", "aa3": "w2c0",
-                 "xx7": "w2c0"}
+                 "xx7": "th2", "hb0": "w3raw1", "hc4": "w4raw1"}
         groups = [(0, 4), (4, 6), (6, 7), (7, 8)]
-        hc, hs, hg = {}, {}, {}
-        for lo, hi in groups:
-            codes = held([P, (hi - lo) * JC], U32, f"hc{lo}")
-            plane = held([P, (hi - lo) * JC], U8, f"hs{lo}")
-            wide = held([P, (hi - lo) * JC, PACK], BF16, f"hb{lo}")
-            hg[hi - 1] = (codes, plane, wide)
-            for u in range(lo, hi):
-                hc[u] = codes[:, (u - lo) * JC:(u - lo + 1) * JC]
-                hs[u] = plane[:, (u - lo) * JC:(u - lo + 1) * JC]
-                hb[u] = wide[:, (u - lo) * JC:(u - lo + 1) * JC, :]
+        hc, hs, hw = {}, {}, {}
 
         def cols(c):
             return slice(c * JC, (c + 1) * JC)
+
+        def parts(u):
+            return [slice(0, JC // 2), slice(JC // 2, JC)] if u == len(units) - 1 else [slice(0, JC)]
 
         def woven(bank):
             return bank[:].rearrange("p t j -> p j t")
@@ -209,28 +203,42 @@ def tile_list_gait_breed_grading_kernel(tc, tab_words, tab_scales, tab2_words, t
                                     lhsT_scale=wscale(w3s, 0, b, t),
                                     rhs=v2w[:, cols(c)].bitcast(FP4X4), rhs_scale=v2s[:, cols(c)], start=True, stop=True)
             xx = held([P, JC, PACK], F32, f"xx{u}", reuse.get(f"xx{u}"))
-            nc.vector.tensor_tensor(out=xx[:], in0=woven(bank), in1=aa[u][:], op=ALU.add)
             ss[u] = held([P, JC, PACK], F32, f"ss{u}", reuse.get(f"ss{u}"))
-            nc.scalar.activation(out=ss[u][:], in_=xx[:], func=ACT.Silu)
+            for js in parts(u):
+                nc.vector.tensor_tensor(out=xx[:, js], in0=woven(bank)[:, js], in1=aa[u][:, js], op=ALU.add)
+            for js in parts(u):
+                nc.scalar.activation(out=ss[u][:, js], in_=xx[:, js], func=ACT.Silu)
 
         def do_gain(u):
             b, c = units[u]
-            eng = nc.gpsimd if u < 6 else nc.vector
-            eng.tensor_tensor(out=hb[u], in0=ss[u][:], in1=gains[:, b, :].unsqueeze(1).to_broadcast([P, JC, PACK]),
-                                    op=ALU.mult)
+            for lo, hi in groups:
+                if u == lo:
+                    hw[lo] = held([P, (hi - lo) * JC, PACK], BF16, f"hb{lo}", reuse.get(f"hb{lo}"))
+                if lo <= u < hi:
+                    hb[u] = hw[lo][:, (u - lo) * JC:(u - lo + 1) * JC, :]
+            eng = nc.gpsimd if u < 5 else nc.vector
+            for js in parts(u):
+                eng.tensor_tensor(out=hb[u][:, js], in0=ss[u][:, js],
+                                  in1=gains[:, b, :].unsqueeze(1).to_broadcast([P, js.stop - js.start, PACK]), op=ALU.mult)
 
-        def do_quant(u):
-            codes, plane, wide = hg[u]
+        def do_quant(lo, hi):
+            codes = held([P, (hi - lo) * JC], U32, f"hc{lo}", reuse.get(f"hc{lo}"))
+            plane = held([P, (hi - lo) * JC], U8, f"hs{lo}")
+            for u in range(lo, hi):
+                hc[u] = codes[:, (u - lo) * JC:(u - lo + 1) * JC]
+                hs[u] = plane[:, (u - lo) * JC:(u - lo + 1) * JC]
+            wide = hw[lo]
             nc.vector.quantize_mx(out=codes[:].bitcast(FP8X4), scales=plane[:], in_=wide[:].rearrange("p j t -> p (j t)"))
 
         w4s = held([P, HALVES * N], U8, "w4s")
         w4q = {}
 
         def round_w4():
-            w4g = held([P, HALVES, N, PACK], BF16, "w4g", "w2c0")
+            w4g = held([P, HALVES, N, PACK], BF16, "w4g", "th2")
             w4q[1] = w4g
             for b in range(HALVES):
-                nc.scalar.copy(out=w4g[:, b], in_=w4raw[b][:].rearrange("p t n -> p n t"))
+                nc.scalar.copy(out=w4g[:, b].rearrange("p (c i) t -> p c t i", i=4),
+                               in_=w4raw[b][:].rearrange("p t (c i) -> p c t i", i=4))
 
         def quantise_w4():
             w4g = w4q[1]
@@ -239,7 +247,7 @@ def tile_list_gait_breed_grading_kernel(tc, tab_words, tab_scales, tab2_words, t
             nc.vector.quantize_mx(out=w4c[:].bitcast(FP8X4), scales=w4s[:], in_=w4g[:].rearrange("p b n t -> p (b n t)"))
 
         def do_out(c):
-            bank = psum.tile([P, N // P, JC], F32, name="ob")
+            bank = psum.tile([P, N // P, JC], F32, name=f"ob{c}", tag="ob" if c < 2 else "sc")
             for b in range(HALVES):
                 for h in range(N // P):
                     u = b * CHUNKS + c
@@ -248,7 +256,10 @@ def tile_list_gait_breed_grading_kernel(tc, tab_words, tab_scales, tab2_words, t
                                         rhs=hc[u].bitcast(FP8X4), rhs_scale=hs[u], start=(b == 0 and h == 0),
                                         stop=(b == HALVES - 1 and h == N // P - 1))
             res = ring.tile([P, N // P, JC], F32, name="res", bufs=4)
-            nc.scalar.copy(out=res[:], in_=bank[:])
+            if c == CHUNKS - 1:
+                nc.vector.tensor_copy(out=res[:], in_=bank[:])
+            else:
+                nc.scalar.copy(out=res[:], in_=bank[:])
             nc.sync.dma_start(out=out.rearrange("(h p) j -> p h j", p=P)[:, :, cols(c)], in_=res[:])
 
         round_w2(0, "w2g0")
@@ -267,30 +278,35 @@ def tile_list_gait_breed_grading_kernel(tc, tab_words, tab_scales, tab2_words, t
         for s in range(n + 3):
             if s == 3:
                 quantise_w2(1, "th2")
-                order_w3(1, "w3c1")
-            if 3 <= s < 3 + CHUNKS:
-                do_tanh(s + 1)
+            if s == 3:
+                do_tanh(4)
+            if s == 4:
+                do_tanh(5)
+                do_tanh(6)
+            if s == 5:
+                do_tanh(7)
             if s < n:
                 do_mul(s)
             if s == 0:
                 gather_words(1, 1)
             if s == 1:
                 order_w1(1, "w1c1")
+                order_w3(1, "w3c1")
             if s == 6:
+                round_w4()
+            if s == 7:
                 quantise_w4()
             if 0 <= s - 1 < n:
                 do_add(s - 1)
-            if s == 4:
-                round_w4()
             if s == 1:
                 turned = psum.tile([P, P], F32, name="sh")
                 nc.tensor.transpose(turned[:], grows[:], ident[:])
                 nc.scalar.copy(out=gains[:].rearrange("p b t -> p (b t)"), in_=turned[:, 0:HALVES * PACK])
             if 0 <= s - 2 < n:
                 do_gain(s - 2)
-            if s - 3 in hg:
-                do_quant(s - 3)
-                for lo, hi in groups:
-                    if hi - 1 == s - 3 and lo >= CHUNKS:
+            for lo, hi in groups:
+                if hi - 1 == s - 3:
+                    do_quant(lo, hi)
+                    if lo >= CHUNKS:
                         for u in range(lo, hi):
                             do_out(u - CHUNKS)

@@ -30,8 +30,12 @@ def tile_list_gait_breed_grading_kernel(tc, tab_words, tab_scales, tab2_words, t
     nc = tc.nc
     with ExitStack() as ctx:
         keep = ctx.enter_context(tc.tile_pool(name="keep", bufs=1))
-        ring = ctx.enter_context(tc.tile_pool(name="ring", bufs=3))
-        psum = ctx.enter_context(tc.psum_pool(name="psum", bufs=2))
+        psum = ctx.enter_context(tc.psum_pool(name="psum", bufs=1))
+        taken = []
+
+        def product_bank(shape):
+            taken.append(shape)
+            return psum.tile(shape, F32, name=f"prod{len(taken)}", tag=f"prod{len(taken) % 4}")
 
         def held(shape, dtype, name, tag=None):
             return keep.tile(shape, dtype, name=name, tag=tag or name, align_bytes=64)
@@ -39,274 +43,245 @@ def tile_list_gait_breed_grading_kernel(tc, tab_words, tab_scales, tab2_words, t
         list1 = held([P, S // 16], U16, "list1")
         list2 = held([P, S // 16], U16, "list2")
         tab2w = held([P, T2], U16, "tab2w")
-        tab2s = held([P, T2], U8, "tab2s")
+        tab2s = held([P, 1, T2], U8, "tab2s")
         tabw = [held([P, T], U32, f"tabw{a}") for a in range(2)]
         tabs = held([P, 2, T], U8, "tabs")
-        w1sraw = held([P, 2, H], U8, "w1sraw")
-        w3sraw = held([P, H], U8, "w3sraw")
+        w1s = held([P, 2, H], U8, "w1s")
+        w3s = held([P, 1, H], U8, "w3s")
         warm = held([P, 2], F32, "warm")
+        ident = held([P, P], F32, "ident")
+        gains = held([P, HALVES, PACK], F32, "gains")
+        w2raw = [held([P, PACK, KP], F32, f"w2raw{b}") for b in range(HALVES)]
+        w1c = [held([P, 2, KP // 2], I32, f"w1c{b}") for b in range(HALVES)]
+        w3c = held([P, H], I32, "w3c")
+        w4raw = [held([P, PACK, N], F32, f"w4raw{b}") for b in range(HALVES)]
 
+        nc.vector.memset(tab2s[:, 0, :].bitcast(I32), 0)
         nc.vector.memset(warm[:, 0:1], 0.0)
         nc.scalar.activation(out=warm[:, 1:2], in_=warm[:, 0:1], func=ACT.Silu)
-        nc.gpsimd.memset(w3sraw[:].bitcast(I32), 0)
-        nc.vector.memset(tab2s[:].bitcast(I32), 0)
+        nc.vector.memset(w3s[:, 0, :].bitcast(I32), 0)
+        nc.vector.memset(w1s[:].rearrange("p a n -> p (a n)").bitcast(I32), 0)
         nc.vector.memset(tabs[:].rearrange("p a n -> p (a n)").bitcast(I32), 0)
-        nc.gpsimd.memset(w1sraw[:].rearrange("p a n -> p (a n)").bitcast(I32), 0)
 
-        w2raw = [[held([P, PACK, KP // 2], F32, f"w2raw{b}{q}") for q in range(2)] for b in range(HALVES)]
-        w1raw = [held([P, 2, KP // 2], I32, f"w1raw{b}") for b in range(HALVES)]
-        w3raw = [held([P, KP], I32, f"w3raw{b}") for b in range(HALVES)]
-        w4raw = [held([P, PACK, N], F32, f"w4raw{b}") for b in range(HALVES)]
-        gains = held([P, HALVES, PACK], F32, "gains")
-        grows = held([P, P], F32, "grows")
-        ident = held([P, P], F32, "ident")
-        nc.vector.memset(grows[:], 0.0)
-
-        def load_w2(b, q):
-            c0 = b * KP + q * KP // 2
-            nc.sync.dma_start(out=w2raw[b][q][:], in_=w2[:, c0:c0 + KP // 2].rearrange("(p j) c -> p j c", j=PACK))
-
-        def load_w3(b):
-            nc.sync.dma_start(out=w3raw[b][:],
-                              in_=w3_words[0].rearrange("p n t -> p (n t)")[:, 4 * KP * b:4 * KP * (b + 1)].bitcast(I32))
+        def load_w2(b):
+            nc.sync.dma_start(out=w2raw[b][:], in_=w2[:, b * KP:(b + 1) * KP].rearrange("(p j) c -> p j c", j=PACK))
 
         def load_w1(b):
-            nc.sync.dma_start(out=w1raw[b][:],
+            nc.sync.dma_start(out=w1c[b][:],
                               in_=w1_words.rearrange("a p n -> p a n")[:, :, 2 * KP * b:2 * KP * (b + 1)].bitcast(I32))
 
-        nc.sync.dma_start(list2[:], offs2)
+        def load_tab(a):
+            nc.sync.dma_start(out=tabw[a][:].bitcast(I32), in_=tab_words[a].rearrange("p n t -> p (n t)").bitcast(I32))
+
+        def scale_rows(eng, plane, scales):
+            for r in range(4):
+                rows = scales[:, r:16:4, :].rearrange("a q n -> q a n").bitcast(I32)
+                eng.dma_start(out=plane[r:P:32].bitcast(I32), in_=rows)
+
         nc.sync.dma_start(out=tab2w[:].bitcast(I32), in_=tab2_words[0].bitcast(I32))
-        for q in range(4):
-            nc.sync.dma_start(out=tab2s[32 * q:32 * q + 4, :].bitcast(I32), in_=tab2_scales[0, 4 * q:4 * q + 4, :].bitcast(I32))
+        nc.sync.dma_start(list2[:], offs2)
+        scale_rows(nc.sync, tab2s[:], tab2_scales)
+        load_w2(0)
+        nc.sync.dma_start(out=w3c[:], in_=w3_words[0].rearrange("p n t -> p (n t)").bitcast(I32))
+        scale_rows(nc.sync, w3s[:], w3_scales)
         nc.sync.dma_start(list1[:], offs)
-        load_w2(0, 0)
-        for q in range(4):
-            nc.sync.dma_start(out=tabs[32 * q:32 * q + 4].bitcast(I32),
-                              in_=tab_scales[:, 4 * q:4 * q + 4, :].rearrange("a r n -> r a n").bitcast(I32))
-        load_w2(0, 1)
-        nc.sync.dma_start(out=tabw[0][:].bitcast(I32), in_=tab_words[0].rearrange("p n t -> p (n t)").bitcast(I32))
-        for q in range(4):
-            nc.sync.dma_start(out=w1sraw[32 * q:32 * q + 4].bitcast(I32),
-                              in_=w1_scales[:, 4 * q:4 * q + 4, :].rearrange("a r n -> r a n").bitcast(I32))
+        load_tab(0)
+        scale_rows(nc.sync, tabs[:], tab_scales)
         load_w1(0)
-        nc.sync.dma_start(out=tabw[1][:].bitcast(I32), in_=tab_words[1].rearrange("p n t -> p (n t)").bitcast(I32))
-        load_w3(0)
-        for q in range(4):
-            nc.sync.dma_start(out=w3sraw[32 * q:32 * q + 4, :].bitcast(I32),
-                              in_=w3_scales[0, 4 * q:4 * q + 4, :].bitcast(I32))
-        load_w2(1, 0)
-        load_w2(1, 1)
-        for b in range(HALVES):
-            nc.sync.dma_start(out=grows[PACK * b:PACK * (b + 1), :].rearrange("t (g i) -> t g i", i=8),
-                              in_=gain[b * KP:(b + 1) * KP].rearrange("(g t i) -> t g i", t=PACK, i=8))
+        load_tab(1)
+        load_w2(1)
         load_w1(1)
-        load_w3(1)
-        make_identity(nc, ident[:])
+        nc.sync.dma_start(out=gains[:], in_=gain.rearrange("(b p t) -> p b t", p=P, t=PACK))
         for b in range(HALVES):
-            rows = w4[b * KP:(b + 1) * KP, :].rearrange("(g t i) n -> t g i n", t=PACK, i=8)
-            for t in range(PACK):
-                nc.sync.dma_start(out=w4raw[b][:, t, :], in_=rows[t])
+            nc.sync.dma_start(out=w4raw[b][:], in_=w4[b * KP:(b + 1) * KP, :].rearrange("(p t) n -> p t n", t=PACK))
+        scale_rows(nc.gpsimd, w1s[:], w1_scales)
+        make_identity(nc, ident[:])
 
         v2w = held([P, S], U16, "v2w")
         v2s = held([P, S], U8, "v2s")
-        nc.vector.tensor_copy(out=v2w[:], in_=tab2w[:].indirect(list2[:]))
-        nc.vector.tensor_copy(out=v2s[:], in_=tab2s[:].indirect(list2[:]))
         vs = [held([P, S], U8, f"vs{a}") for a in range(2)]
-        for a in range(2):
-            nc.vector.tensor_copy(out=vs[a][:], in_=tabs[:, a, :].indirect(list1[:]))
-
-        w2g, w2c = {}, {}
-        w2s = [held([P, KP], U8, f"w2s{b}") for b in range(HALVES)]
-
-        def round_w2(b, rounded_tag):
-            w2g[b] = held([P, KP * PACK], BF16, f"w2g{b}", rounded_tag)
-            dst = w2g[b][:].rearrange("p (t q g i j) -> p q t g i j", t=PACK, q=2, i=8, j=PACK)
-            for q in range(2):
-                nc.scalar.copy(out=dst[:, q], in_=w2raw[b][q][:].rearrange("p j (g t i) -> p t g i j", t=PACK, i=8))
-
-        def quantise_w2(b, codes_tag):
-            w2c[b] = held([P, KP], U32, f"w2c{b}", codes_tag)
-            nc.vector.quantize_mx(out=w2c[b][:].bitcast(FP8X4), scales=w2s[b][:], in_=w2g[b][:])
-
-        w1s = held([P, 2 * H // 4], I32, "w1s")
-        w3s = held([P, H // 4], I32, "w3s")
-        w1c, w3c = {}, {}
-
-        def order_scales(dst, raw):
-            nc.vector.tensor_copy(out=dst[:].rearrange("p (a t g w) -> p a t g w", t=PACK, g=16, w=2),
-                                  in_=raw.bitcast(I32).rearrange("p (a g t w) -> p a t g w", t=PACK, g=16, w=2))
-
-        def order_w3(b, tag):
-            w3c[b] = held([P, KP], I32, f"w3c{b}", tag)
-            nc.gpsimd.tensor_copy(out=w3c[b][:].rearrange("p (t g w) -> p t g w", t=PACK, w=8),
-                                  in_=w3raw[b][:].rearrange("p (g t w) -> p t g w", t=PACK, w=8))
-
-        def order_w1(b, tag):
-            w1c[b] = held([P, 2, KP // 2], I32, f"w1c{b}", tag)
-            for a in range(2):
-                nc.gpsimd.tensor_copy(out=w1c[b][:, a, :].rearrange("p (t g w) -> p t g w", t=PACK, w=4),
-                                      in_=w1raw[b][:, a, :].rearrange("p (g t w) -> p t g w", t=PACK, w=4))
-
-        def wscale(plane, a, b, t):
-            c0 = (a * H + b * KP + t * P) // 4
-            return plane[:, c0:c0 + P // 4].bitcast(U8)
-
-        vw = [[held([P, S // 2], U32, f"vw{a}{q}") for q in range(2)] for a in range(2)]
-
-        def gather_words(a, q):
-            nc.vector.tensor_copy(out=vw[a][q][:], in_=tabw[a][:].indirect(list1[:, 16 * q:16 * (q + 1)]))
-
-        units = [(b, c) for b in range(HALVES) for c in range(CHUNKS)]
-        th, aa, ss, hb = {}, {}, {}, {}
-        reuse = {"ss0": "w2raw10", "ss1": "w2raw11", "ss5": "w4raw0", "ss6": "w4raw1", "aa3": "w2c0",
-                 "xx7": "th2", "hb0": "w3raw1", "hc4": "w4raw1"}
-        groups = [(0, 4), (4, 6), (6, 7), (7, 8)]
-        hc, hs, hw = {}, {}, {}
+        vw1 = {}
 
         def cols(c):
             return slice(c * JC, (c + 1) * JC)
 
-        def parts(u):
-            return [slice(0, JC // 2), slice(JC // 2, JC)] if u == len(units) - 1 else [slice(0, JC)]
+        def weave(eng, dst, raw):
+            d = dst.rearrange("p (c i) t -> p c t i", i=4)
+            s = raw.rearrange("p t (c i) -> p c t i", i=4)
+            if eng is nc.scalar:
+                nc.scalar.copy(out=d, in_=s)
+            elif eng is nc.gpsimd:
+                nc.gpsimd.tensor_scalar(out=dst, in0=raw.rearrange("p t c -> p c t"), scalar1=1.0, scalar2=0.0,
+                                        op0=ALU.mult, op1=ALU.add)
+            else:
+                nc.vector.tensor_copy(out=d, in_=s)
 
-        def woven(bank):
-            return bank[:].rearrange("p t j -> p j t")
+        w2g = {}
+        w2c = [held([P, KP], U32, f"w2c{b}") for b in range(HALVES)]
+        w2s = [held([P, KP], U8, f"w2s{b}") for b in range(HALVES)]
+
+        def round_w2(b, q, eng):
+            half = slice(q * KP // 2, (q + 1) * KP // 2)
+            weave(eng, w2g[b][:, half], w2raw[b][:, :, half])
+
+        def quantise_w2(b):
+            nc.vector.quantize_mx(out=w2c[b][:].bitcast(FP8X4), scales=w2s[b][:], in_=w2g[b][:].rearrange("p c t -> p (c t)"))
+
+        units = [(b, c) for b in range(HALVES) for c in range(CHUNKS)]
+        th, sh, xt, ss, hb = {}, {}, {}, {}, {}
+        groups = [(0, 4), (4, 6), (6, 7), (7, 8)]
+        hc, hs, hw = {}, {}, {}
+
+        def planes(bank):
+            return bank[:].rearrange("p (q t) -> p t q", t=PACK)
 
         def do_tanh(u):
             b, c = units[u]
-            bank = psum.tile([P, PACK, JC], F32, name="sc")
+            bank = product_bank([P, KP])
+            nc.tensor.matmul_mx(out=bank[:], lhsT=v2w[:, cols(c)].bitcast(FP4X4), lhsT_scale=v2s[:, cols(c)],
+                                rhs=w2c[b][:].bitcast(FP8X4), rhs_scale=w2s[b][:], start=True, stop=True)
+            th[u] = held([P, PACK, P], F32, f"th{u}")
+            nc.scalar.activation(out=th[u][:], in_=planes(bank), func=ACT.Tanh)
+
+        def do_shift(u):
+            b, c = units[u]
+            bank = product_bank([P, KP])
+            nc.tensor.matmul_mx(out=bank[:], lhsT=v2w[:, cols(c)].bitcast(FP4X4), lhsT_scale=v2s[:, cols(c)],
+                                rhs=w3c[:, b * KP:(b + 1) * KP].bitcast(FP8X4), rhs_scale=w3s[:, 0, b * KP:(b + 1) * KP], start=True, stop=True)
+            sh[u] = held([P, PACK, P], F32, f"sh{u}")
+            nc.scalar.copy(out=sh[u][:], in_=planes(bank))
+
+        def turn_shift(u):
+            xt[u] = psum.tile([P, PACK, JC], F32, name=f"xt{u}", tag=f"xt{u % 4}")
             for t in range(PACK):
-                nc.tensor.matmul_mx(out=bank[:, t, :], lhsT=w2c[b][:, t * P:(t + 1) * P].bitcast(FP8X4),
-                                    lhsT_scale=w2s[b][:, t * P:(t + 1) * P],
-                                    rhs=v2w[:, cols(c)].bitcast(FP4X4), rhs_scale=v2s[:, cols(c)], start=True, stop=True)
-            th[u] = held([P, JC, PACK], F32, f"th{u}")
-            nc.scalar.activation(out=th[u][:], in_=woven(bank), func=ACT.Tanh)
+                nc.tensor.matmul(xt[u][:, t, :], sh[u][:, t, :], ident[:], start=(t == 0), stop=False, is_transpose=True)
+
+        def do_motion(u):
+            b, c = units[u]
+            bank = product_bank([P, KP])
+            mo[u] = bank
+            for a in range(2):
+                words = vw0[:, cols(c)] if a == 0 else vw1[c // 2][:, cols(c % 2)]
+                nc.tensor.matmul_mx(out=bank[:], lhsT=words.bitcast(FP8X4), lhsT_scale=vs[a][:, cols(c)],
+                                    rhs=w1c[b][:, a, :].bitcast(FP4X4), rhs_scale=w1s[:, a, b * KP:(b + 1) * KP],
+                                    start=(a == 0), stop=(a == 1))
 
         def do_mul(u):
-            b, c = units[u]
-            bank = psum.tile([P, PACK, JC], F32, name="mo")
-            for a in range(2):
-                for t in range(PACK):
-                    nc.tensor.matmul_mx(out=bank[:, t, :],
-                                        lhsT=w1c[b][:, a, t * P // 2:(t + 1) * P // 2].bitcast(FP4X4),
-                                        lhsT_scale=wscale(w1s, a, b, t),
-                                        rhs=vw[a][c // 2][:, cols(c % 2)].bitcast(FP8X4), rhs_scale=vs[a][:, cols(c)],
-                                        start=(a == 0 and t == 0), stop=(a == 1 and t == PACK - 1))
-            aa[u] = held([P, JC, PACK], F32, f"aa{u}", reuse.get(f"aa{u}"))
-            nc.vector.scalar_tensor_tensor(out=aa[u][:], in0=th[u][:], scalar=1.0, in1=woven(bank), op0=ALU.add, op1=ALU.mult)
-
-        def do_add(u):
-            b, c = units[u]
-            bank = psum.tile([P, PACK, JC], F32, name="sh")
+            bank = mo[u]
+            aa = held([P, PACK, P], F32, f"aa{u}")
+            nc.vector.scalar_tensor_tensor(out=aa[:], in0=th[u][:], scalar=1.0, in1=planes(bank), op0=ALU.add, op1=ALU.mult)
             for t in range(PACK):
-                nc.tensor.matmul_mx(out=bank[:, t, :], lhsT=w3c[b][:, t * P:(t + 1) * P].bitcast(FP8X4),
-                                    lhsT_scale=wscale(w3s, 0, b, t),
-                                    rhs=v2w[:, cols(c)].bitcast(FP4X4), rhs_scale=v2s[:, cols(c)], start=True, stop=True)
-            xx = held([P, JC, PACK], F32, f"xx{u}", reuse.get(f"xx{u}"))
-            ss[u] = held([P, JC, PACK], F32, f"ss{u}", reuse.get(f"ss{u}"))
+                nc.tensor.matmul(xt[u][:, t, :], aa[:, t, :], ident[:], start=False, stop=(t == PACK - 1), is_transpose=True)
+
+        def parts(u):
+            return [slice(0, JC // 2), slice(JC // 2, JC)] if u == len(units) - 1 else [slice(0, JC)]
+
+        def do_silu(u):
+            ss[u] = held([P, JC, PACK], F32, f"ss{u}")
             for js in parts(u):
-                nc.vector.tensor_tensor(out=xx[:, js], in0=woven(bank)[:, js], in1=aa[u][:, js], op=ALU.add)
-            for js in parts(u):
-                nc.scalar.activation(out=ss[u][:, js], in_=xx[:, js], func=ACT.Silu)
+                nc.scalar.activation(out=ss[u][:, js], in_=xt[u][:].rearrange("p t j -> p j t")[:, js], func=ACT.Silu)
 
         def do_gain(u):
             b, c = units[u]
             for lo, hi in groups:
                 if u == lo:
-                    hw[lo] = held([P, (hi - lo) * JC, PACK], BF16, f"hb{lo}", reuse.get(f"hb{lo}"))
+                    hw[lo] = held([P, (hi - lo) * JC, PACK], BF16, f"hb{lo}")
                 if lo <= u < hi:
                     hb[u] = hw[lo][:, (u - lo) * JC:(u - lo + 1) * JC, :]
-            eng = nc.gpsimd if u < 5 else nc.vector
             for js in parts(u):
-                eng.tensor_tensor(out=hb[u][:, js], in0=ss[u][:, js],
-                                  in1=gains[:, b, :].unsqueeze(1).to_broadcast([P, js.stop - js.start, PACK]), op=ALU.mult)
+                nc.vector.tensor_tensor(out=hb[u][:, js], in0=ss[u][:, js],
+                                        in1=gains[:, b, :].unsqueeze(1).to_broadcast([P, js.stop - js.start, PACK]), op=ALU.mult)
 
         def do_quant(lo, hi):
-            codes = held([P, (hi - lo) * JC], U32, f"hc{lo}", reuse.get(f"hc{lo}"))
+            codes = held([P, (hi - lo) * JC], U32, f"hc{lo}")
             plane = held([P, (hi - lo) * JC], U8, f"hs{lo}")
             for u in range(lo, hi):
                 hc[u] = codes[:, (u - lo) * JC:(u - lo + 1) * JC]
                 hs[u] = plane[:, (u - lo) * JC:(u - lo + 1) * JC]
-            wide = hw[lo]
-            nc.vector.quantize_mx(out=codes[:].bitcast(FP8X4), scales=plane[:], in_=wide[:].rearrange("p j t -> p (j t)"))
+            nc.vector.quantize_mx(out=codes[:].bitcast(FP8X4), scales=plane[:], in_=hw[lo][:].rearrange("p j t -> p (j t)"))
 
         w4s = held([P, HALVES * N], U8, "w4s")
-        w4q = {}
+        w4c = held([P, HALVES * N], U32, "w4c")
 
-        def round_w4():
-            w4g = held([P, HALVES, N, PACK], BF16, "w4g", "th2")
-            w4q[1] = w4g
+        def prepare_w4():
+            w4g = held([P, HALVES, N, PACK], BF16, "w4g", "aa4")
             for b in range(HALVES):
-                nc.scalar.copy(out=w4g[:, b].rearrange("p (c i) t -> p c t i", i=4),
-                               in_=w4raw[b][:].rearrange("p t (c i) -> p c t i", i=4))
-
-        def quantise_w4():
-            w4g = w4q[1]
-            w4c = held([P, HALVES * N], U32, "w4c", "th5")
-            w4q[0] = w4c
+                weave(nc.scalar, w4g[:, b], w4raw[b][:])
             nc.vector.quantize_mx(out=w4c[:].bitcast(FP8X4), scales=w4s[:], in_=w4g[:].rearrange("p b n t -> p (b n t)"))
 
         def do_out(c):
-            bank = psum.tile([P, N // P, JC], F32, name=f"ob{c}", tag="ob" if c < 2 else "sc")
+            bank = product_bank([P, N // P, JC])
             for b in range(HALVES):
                 for h in range(N // P):
                     u = b * CHUNKS + c
                     w = slice(b * N + h * P, b * N + (h + 1) * P)
-                    nc.tensor.matmul_mx(out=bank[:, h, :], lhsT=w4q[0][:, w].bitcast(FP8X4), lhsT_scale=w4s[:, w],
+                    nc.tensor.matmul_mx(out=bank[:, h, :], lhsT=w4c[:, w].bitcast(FP8X4), lhsT_scale=w4s[:, w],
                                         rhs=hc[u].bitcast(FP8X4), rhs_scale=hs[u], start=(b == 0 and h == 0),
                                         stop=(b == HALVES - 1 and h == N // P - 1))
-            res = ring.tile([P, N // P, JC], F32, name="res", bufs=4)
+            res = held([P, N // P, JC], F32, f"res{c}")
             if c == CHUNKS - 1:
                 nc.vector.tensor_copy(out=res[:], in_=bank[:])
             else:
                 nc.scalar.copy(out=res[:], in_=bank[:])
             nc.sync.dma_start(out=out.rearrange("(h p) j -> p h j", p=P)[:, :, cols(c)], in_=res[:])
 
-        round_w2(0, "w2g0")
-        quantise_w2(0, "w2c0")
+        nc.vector.tensor_copy(out=v2w[:], in_=tab2w[:].indirect(list2[:]))
+        nc.vector.tensor_copy(out=v2s[:], in_=tab2s[:, 0, :].indirect(list2[:]))
+        w2g[0] = held([P, KP, PACK], BF16, "w2g0")
+        round_w2(0, 0, nc.scalar)
+        round_w2(0, 1, nc.vector)
+        quantise_w2(0)
+        for pair in ((0, 1), (2, 3)):
+            for u in pair:
+                do_shift(u)
+                turn_shift(u)
+            for u in pair:
+                do_tanh(u)
+        vw0 = held([P, S], U32, "vw0", "w2g0")
+        nc.vector.tensor_copy(out=vw0[:], in_=tabw[0][:].indirect(list1[:]))
+        for a in range(2):
+            nc.vector.tensor_copy(out=vs[a][:], in_=tabs[:, a, :].indirect(list1[:]))
+        vw1[0] = held([P, S // 2], U32, "vw10")
+        nc.vector.tensor_copy(out=vw1[0][:], in_=tabw[1][:].indirect(list1[:, 0:16]))
+        mo = {}
         for u in range(CHUNKS):
-            do_tanh(u)
-        gather_words(0, 0)
-        gather_words(0, 1)
-        order_scales(w1s, w1sraw[:].rearrange("p a n -> p (a n)"))
-        order_w1(0, "w1c0")
-        gather_words(1, 0)
-        order_w3(0, "w3c0")
-        order_scales(w3s, w3sraw[:])
-        n = len(units)
-        round_w2(1, "w2c0")
-        for s in range(n + 3):
-            if s == 3:
-                quantise_w2(1, "th2")
-            if s == 3:
-                do_tanh(4)
-            if s == 4:
-                do_tanh(5)
-                do_tanh(6)
-            if s == 5:
-                do_tanh(7)
-            if s < n:
-                do_mul(s)
-            if s == 0:
-                gather_words(1, 1)
-            if s == 1:
-                order_w1(1, "w1c1")
-                order_w3(1, "w3c1")
-            if s == 6:
-                round_w4()
-            if s == 7:
-                quantise_w4()
-            if 0 <= s - 1 < n:
-                do_add(s - 1)
-            if s == 1:
-                turned = psum.tile([P, P], F32, name="sh")
-                nc.tensor.transpose(turned[:], grows[:], ident[:])
-                nc.scalar.copy(out=gains[:].rearrange("p b t -> p (b t)"), in_=turned[:, 0:HALVES * PACK])
-            if 0 <= s - 2 < n:
-                do_gain(s - 2)
-            for lo, hi in groups:
-                if hi - 1 == s - 3:
-                    do_quant(lo, hi)
-                    if lo >= CHUNKS:
-                        for u in range(lo, hi):
-                            do_out(u - CHUNKS)
+            do_motion(u)
+            if u % 2 == 1:
+                do_shift(u + 3)
+                do_shift(u + 4)
+            do_mul(u)
+            if u == 0:
+                vw1[1] = held([P, S // 2], U32, "vw11")
+                nc.vector.tensor_copy(out=vw1[1][:], in_=tabw[1][:].indirect(list1[:, 16:32]))
+                do_silu(0)
+                w2g[1] = held([P, KP, PACK], BF16, "w2g1", "aa0")
+                round_w2(1, 0, nc.scalar)
+                round_w2(1, 1, nc.gpsimd)
+        quantise_w2(1)
+        do_silu(1)
+        do_silu(2)
+        do_tanh(4)
+        do_silu(3)
+        do_gain(0)
+        do_gain(1)
+        for u in range(CHUNKS, 2 * CHUNKS):
+            turn_shift(u)
+            if u + 1 < 2 * CHUNKS:
+                do_tanh(u + 1)
+            if u > CHUNKS:
+                do_silu(u - 1)
+            do_motion(u)
+            do_mul(u)
+            do_gain(u - 2)
+            if u == 5:
+                do_quant(0, 4)
+            if u == 6:
+                prepare_w4()
+        do_silu(7)
+        do_quant(4, 6)
+        do_out(0)
+        do_out(1)
+        for u in (6, 7):
+            do_gain(u)
+            do_quant(u, u + 1)
+            do_out(u - CHUNKS)

@@ -53,7 +53,7 @@ def tile_list_gait_breed_grading_kernel(tc, tab_words, tab_scales, tab2_words, t
         gains = held([P, HALVES, PACK], F32, "gains")
         w2raw = [held([P, PACK, KP], F32, f"w2raw{b}") for b in range(HALVES)]
         w1c = [held([P, 2, KP // 2], I32, f"w1c{b}") for b in range(HALVES)]
-        w3c = held([P, H], I32, "w3c")
+        w3c = [held([P, KP], I32, f"w3c{b}") for b in range(HALVES)]
         w4raw = [held([P, PACK, N], F32, f"w4raw{b}") for b in range(HALVES)]
 
         nc.vector.memset(tab2s[:, 0, :].bitcast(I32), 0)
@@ -65,6 +65,10 @@ def tile_list_gait_breed_grading_kernel(tc, tab_words, tab_scales, tab2_words, t
 
         def load_w2(b):
             nc.sync.dma_start(out=w2raw[b][:], in_=w2[:, b * KP:(b + 1) * KP].rearrange("(p j) c -> p j c", j=PACK))
+
+        def load_w3(b):
+            nc.sync.dma_start(out=w3c[b][:],
+                              in_=w3_words[0].rearrange("p n t -> p (n t)")[:, 4 * KP * b:4 * KP * (b + 1)].bitcast(I32))
 
         def load_w1(b):
             nc.sync.dma_start(out=w1c[b][:],
@@ -81,20 +85,21 @@ def tile_list_gait_breed_grading_kernel(tc, tab_words, tab_scales, tab2_words, t
         nc.sync.dma_start(out=tab2w[:].bitcast(I32), in_=tab2_words[0].bitcast(I32))
         nc.sync.dma_start(list2[:], offs2)
         scale_rows(nc.sync, tab2s[:], tab2_scales)
+        load_w3(0)
         load_w2(0)
-        nc.sync.dma_start(out=w3c[:], in_=w3_words[0].rearrange("p n t -> p (n t)").bitcast(I32))
         scale_rows(nc.sync, w3s[:], w3_scales)
         nc.sync.dma_start(list1[:], offs)
         load_tab(0)
         scale_rows(nc.sync, tabs[:], tab_scales)
         load_w1(0)
         load_tab(1)
+        scale_rows(nc.sync, w1s[:], w1_scales)
+        load_w3(1)
         load_w2(1)
         load_w1(1)
         nc.sync.dma_start(out=gains[:], in_=gain.rearrange("(b p t) -> p b t", p=P, t=PACK))
         for b in range(HALVES):
             nc.sync.dma_start(out=w4raw[b][:], in_=w4[b * KP:(b + 1) * KP, :].rearrange("(p t) n -> p t n", t=PACK))
-        scale_rows(nc.gpsimd, w1s[:], w1_scales)
         make_identity(nc, ident[:])
 
         v2w = held([P, S], U16, "v2w")
@@ -110,9 +115,6 @@ def tile_list_gait_breed_grading_kernel(tc, tab_words, tab_scales, tab2_words, t
             s = raw.rearrange("p t (c i) -> p c t i", i=4)
             if eng is nc.scalar:
                 nc.scalar.copy(out=d, in_=s)
-            elif eng is nc.gpsimd:
-                nc.gpsimd.tensor_scalar(out=dst, in0=raw.rearrange("p t c -> p c t"), scalar1=1.0, scalar2=0.0,
-                                        op0=ALU.mult, op1=ALU.add)
             else:
                 nc.vector.tensor_copy(out=d, in_=s)
 
@@ -147,7 +149,7 @@ def tile_list_gait_breed_grading_kernel(tc, tab_words, tab_scales, tab2_words, t
             b, c = units[u]
             bank = product_bank([P, KP])
             nc.tensor.matmul_mx(out=bank[:], lhsT=v2w[:, cols(c)].bitcast(FP4X4), lhsT_scale=v2s[:, cols(c)],
-                                rhs=w3c[:, b * KP:(b + 1) * KP].bitcast(FP8X4), rhs_scale=w3s[:, 0, b * KP:(b + 1) * KP], start=True, stop=True)
+                                rhs=w3c[b][:].bitcast(FP8X4), rhs_scale=w3s[:, 0, b * KP:(b + 1) * KP], start=True, stop=True)
             sh[u] = held([P, PACK, P], F32, f"sh{u}")
             nc.scalar.copy(out=sh[u][:], in_=planes(bank))
 
@@ -169,7 +171,9 @@ def tile_list_gait_breed_grading_kernel(tc, tab_words, tab_scales, tab2_words, t
         def do_mul(u):
             bank = mo[u]
             aa = held([P, PACK, P], F32, f"aa{u}")
-            nc.vector.scalar_tensor_tensor(out=aa[:], in0=th[u][:], scalar=1.0, in1=planes(bank), op0=ALU.add, op1=ALU.mult)
+            for ts in ([slice(0, 2), slice(2, 4)] if u == len(units) - 1 else [slice(0, PACK)]):
+                nc.vector.scalar_tensor_tensor(out=aa[:, ts], in0=th[u][:, ts], scalar=1.0, in1=planes(bank)[:, ts],
+                                               op0=ALU.add, op1=ALU.mult)
             for t in range(PACK):
                 nc.tensor.matmul(xt[u][:, t, :], aa[:, t, :], ident[:], start=False, stop=(t == PACK - 1), is_transpose=True)
 
@@ -209,6 +213,20 @@ def tile_list_gait_breed_grading_kernel(tc, tab_words, tab_scales, tab2_words, t
                 weave(nc.scalar, w4g[:, b], w4raw[b][:])
             nc.vector.quantize_mx(out=w4c[:].bitcast(FP8X4), scales=w4s[:], in_=w4g[:].rearrange("p b n t -> p (b n t)"))
 
+        def do_last_out(c):
+            banks = [product_bank([P, JC]), psum.tile([P, JC], F32, name="last", tag="xt0")]
+            for b in range(HALVES):
+                for h in range(N // P):
+                    u = b * CHUNKS + c
+                    w = slice(b * N + h * P, b * N + (h + 1) * P)
+                    nc.tensor.matmul_mx(out=banks[h][:], lhsT=w4c[:, w].bitcast(FP8X4), lhsT_scale=w4s[:, w],
+                                        rhs=hc[u].bitcast(FP8X4), rhs_scale=hs[u], start=(b == 0), stop=(b == HALVES - 1))
+            res = [held([P, JC], F32, f"last{h}") for h in range(N // P)]
+            nc.vector.tensor_copy(out=res[0][:], in_=banks[0][:])
+            nc.sync.dma_start(out=out[0:P, cols(c)], in_=res[0][:])
+            nc.scalar.copy(out=res[1][:], in_=banks[1][:])
+            nc.scalar.dma_start(out=out[P:2 * P, cols(c)], in_=res[1][:])
+
         def do_out(c):
             bank = product_bank([P, N // P, JC])
             for b in range(HALVES):
@@ -219,10 +237,7 @@ def tile_list_gait_breed_grading_kernel(tc, tab_words, tab_scales, tab2_words, t
                                         rhs=hc[u].bitcast(FP8X4), rhs_scale=hs[u], start=(b == 0 and h == 0),
                                         stop=(b == HALVES - 1 and h == N // P - 1))
             res = held([P, N // P, JC], F32, f"res{c}")
-            if c == CHUNKS - 1:
-                nc.vector.tensor_copy(out=res[:], in_=bank[:])
-            else:
-                nc.scalar.copy(out=res[:], in_=bank[:])
+            nc.scalar.copy(out=res[:], in_=bank[:])
             nc.sync.dma_start(out=out.rearrange("(h p) j -> p h j", p=P)[:, :, cols(c)], in_=res[:])
 
         nc.vector.tensor_copy(out=v2w[:], in_=tab2w[:].indirect(list2[:]))
@@ -231,12 +246,11 @@ def tile_list_gait_breed_grading_kernel(tc, tab_words, tab_scales, tab2_words, t
         round_w2(0, 0, nc.scalar)
         round_w2(0, 1, nc.vector)
         quantise_w2(0)
-        for pair in ((0, 1), (2, 3)):
-            for u in pair:
-                do_shift(u)
-                turn_shift(u)
-            for u in pair:
-                do_tanh(u)
+        for u in range(CHUNKS):
+            do_shift(u)
+            turn_shift(u)
+        for u in range(CHUNKS):
+            do_tanh(u)
         vw0 = held([P, S], U32, "vw0", "w2g0")
         nc.vector.tensor_copy(out=vw0[:], in_=tabw[0][:].indirect(list1[:]))
         for a in range(2):
@@ -256,7 +270,7 @@ def tile_list_gait_breed_grading_kernel(tc, tab_words, tab_scales, tab2_words, t
                 do_silu(0)
                 w2g[1] = held([P, KP, PACK], BF16, "w2g1", "aa0")
                 round_w2(1, 0, nc.scalar)
-                round_w2(1, 1, nc.gpsimd)
+        round_w2(1, 1, nc.vector)
         quantise_w2(1)
         do_silu(1)
         do_silu(2)
@@ -281,7 +295,9 @@ def tile_list_gait_breed_grading_kernel(tc, tab_words, tab_scales, tab2_words, t
         do_quant(4, 6)
         do_out(0)
         do_out(1)
-        for u in (6, 7):
-            do_gain(u)
-            do_quant(u, u + 1)
-            do_out(u - CHUNKS)
+        do_gain(6)
+        do_quant(6, 7)
+        do_out(2)
+        do_gain(7)
+        do_quant(7, 8)
+        do_last_out(3)

@@ -30,12 +30,13 @@ def tile_list_gait_breed_grading_kernel(tc, tab_words, tab_scales, tab2_words, t
     nc = tc.nc
     with ExitStack() as ctx:
         keep = ctx.enter_context(tc.tile_pool(name="keep", bufs=1))
+        shared = ctx.enter_context(tc.tile_pool(name="shared", bufs=1))
         psum = ctx.enter_context(tc.psum_pool(name="psum", bufs=1))
         taken = []
 
-        def product_bank(shape):
+        def product_bank(shape, which=None):
             taken.append(shape)
-            return psum.tile(shape, F32, name=f"prod{len(taken)}", tag=f"prod{len(taken) % 4}")
+            return psum.tile(shape, F32, name=f"prod{len(taken)}", tag=f"prod{len(taken) % 4 if which is None else which}")
 
         def held(shape, dtype, name, tag=None):
             return keep.tile(shape, dtype, name=name, tag=tag or name, align_bytes=64)
@@ -44,31 +45,30 @@ def tile_list_gait_breed_grading_kernel(tc, tab_words, tab_scales, tab2_words, t
         list2 = held([P, S // 16], U16, "list2")
         tab2w = held([P, T2], U16, "tab2w")
         tab2s = held([P, 1, T2], U8, "tab2s")
-        tabw = [held([P, T], U32, f"tabw{a}") for a in range(2)]
-        tabs = held([P, 2, T], U8, "tabs")
+        tabw = [shared.tile([P, T], U32, name="tabw0", offset=0), held([P, T], U32, "tabw1")]
+        tabs = held([P, T], U8, "tabs")
+        vs = {1: held([P, S], U8, "vs1")}
         w1s = held([P, 2, H], U8, "w1s")
         w3s = held([P, 1, H], U8, "w3s")
         warm = held([P, 2], F32, "warm")
         ident = held([P, P], F32, "ident")
         gains = held([P, HALVES, PACK], F32, "gains")
-        w2raw = [held([P, PACK, KP], F32, f"w2raw{b}") for b in range(HALVES)]
-        w1c = [held([P, 2, KP // 2], I32, f"w1c{b}") for b in range(HALVES)]
-        w3c = [held([P, KP], I32, f"w3c{b}") for b in range(HALVES)]
-        w4raw = [held([P, PACK, N], F32, f"w4raw{b}") for b in range(HALVES)]
+        w2first = [held([P, PACK, KP // 2], F32, f"w2first{q}") for q in range(2)]
+        w1c = {0: held([P, 2, KP // 2], I32, "w1c0")}
+        w3c = held([P, H], I32, "w3c")
 
         nc.vector.memset(tab2s[:, 0, :].bitcast(I32), 0)
         nc.vector.memset(warm[:, 0:1], 0.0)
         nc.scalar.activation(out=warm[:, 1:2], in_=warm[:, 0:1], func=ACT.Silu)
         nc.vector.memset(w3s[:, 0, :].bitcast(I32), 0)
+        nc.vector.memset(tabs[:].bitcast(I32), 0)
         nc.vector.memset(w1s[:].rearrange("p a n -> p (a n)").bitcast(I32), 0)
-        nc.vector.memset(tabs[:].rearrange("p a n -> p (a n)").bitcast(I32), 0)
+        nc.vector.memset(vs[1][:].bitcast(I32), 0)
 
-        def load_w2(b):
-            nc.sync.dma_start(out=w2raw[b][:], in_=w2[:, b * KP:(b + 1) * KP].rearrange("(p j) c -> p j c", j=PACK))
+        def load_w2(tile, first):
+            width = tile.shape[2]
+            nc.sync.dma_start(out=tile[:], in_=w2[:, first:first + width].rearrange("(p j) c -> p j c", j=PACK))
 
-        def load_w3(b):
-            nc.sync.dma_start(out=w3c[b][:],
-                              in_=w3_words[0].rearrange("p n t -> p (n t)")[:, 4 * KP * b:4 * KP * (b + 1)].bitcast(I32))
 
         def load_w1(b):
             nc.sync.dma_start(out=w1c[b][:],
@@ -85,26 +85,22 @@ def tile_list_gait_breed_grading_kernel(tc, tab_words, tab_scales, tab2_words, t
         nc.sync.dma_start(out=tab2w[:].bitcast(I32), in_=tab2_words[0].bitcast(I32))
         nc.sync.dma_start(list2[:], offs2)
         scale_rows(nc.sync, tab2s[:], tab2_scales)
-        load_w3(0)
-        load_w2(0)
+        nc.sync.dma_start(out=w3c[:], in_=w3_words[0].rearrange("p n t -> p (n t)").bitcast(I32))
+        load_w2(w2first[0], 0)
         scale_rows(nc.sync, w3s[:], w3_scales)
+        load_w2(w2first[1], KP // 2)
         nc.sync.dma_start(list1[:], offs)
+        for r in range(4):
+            nc.sync.dma_start(out=tabs[r:P:16].bitcast(I32), in_=tab_scales[:, r:16:4, :].rearrange("a q n -> q a n").bitcast(I32))
         load_tab(0)
-        scale_rows(nc.sync, tabs[:], tab_scales)
         load_w1(0)
-        load_tab(1)
         scale_rows(nc.sync, w1s[:], w1_scales)
-        load_w3(1)
-        load_w2(1)
-        load_w1(1)
+        load_tab(1)
         nc.sync.dma_start(out=gains[:], in_=gain.rearrange("(b p t) -> p b t", p=P, t=PACK))
-        for b in range(HALVES):
-            nc.sync.dma_start(out=w4raw[b][:], in_=w4[b * KP:(b + 1) * KP, :].rearrange("(p t) n -> p t n", t=PACK))
         make_identity(nc, ident[:])
 
         v2w = held([P, S], U16, "v2w")
         v2s = held([P, S], U8, "v2s")
-        vs = [held([P, S], U8, f"vs{a}") for a in range(2)]
         vw1 = {}
 
         def cols(c):
@@ -124,7 +120,7 @@ def tile_list_gait_breed_grading_kernel(tc, tab_words, tab_scales, tab2_words, t
 
         def round_w2(b, q, eng):
             half = slice(q * KP // 2, (q + 1) * KP // 2)
-            weave(eng, w2g[b][:, half], w2raw[b][:, :, half])
+            weave(eng, w2g[b][:, half], w2second[:, :, half] if b else w2first[q][:])
 
         def quantise_w2(b):
             nc.vector.quantize_mx(out=w2c[b][:].bitcast(FP8X4), scales=w2s[b][:], in_=w2g[b][:].rearrange("p c t -> p (c t)"))
@@ -139,38 +135,40 @@ def tile_list_gait_breed_grading_kernel(tc, tab_words, tab_scales, tab2_words, t
 
         def do_tanh(u):
             b, c = units[u]
-            bank = product_bank([P, KP])
+            bank = psum.tile([P, KP], F32, name=f"scale{u}", tag=f"xt{u - 6}") if u >= 6 else product_bank([P, KP], c + 2 * b)
             nc.tensor.matmul_mx(out=bank[:], lhsT=v2w[:, cols(c)].bitcast(FP4X4), lhsT_scale=v2s[:, cols(c)],
                                 rhs=w2c[b][:].bitcast(FP8X4), rhs_scale=w2s[b][:], start=True, stop=True)
-            th[u] = held([P, PACK, P], F32, f"th{u}")
+            th[u] = held([P, PACK, P], F32, f"th{u}") if u else shared.tile([P, PACK, P], F32, name="th0", offset=16384)
             nc.scalar.activation(out=th[u][:], in_=planes(bank), func=ACT.Tanh)
 
         def do_shift(u):
             b, c = units[u]
-            bank = product_bank([P, KP])
+            bank = psum.tile([P, KP], F32, name=f"shift{u}", tag=f"xt{c}") if b else product_bank([P, KP], c)
             nc.tensor.matmul_mx(out=bank[:], lhsT=v2w[:, cols(c)].bitcast(FP4X4), lhsT_scale=v2s[:, cols(c)],
-                                rhs=w3c[b][:].bitcast(FP8X4), rhs_scale=w3s[:, 0, b * KP:(b + 1) * KP], start=True, stop=True)
+                                rhs=w3c[:, b * KP:(b + 1) * KP].bitcast(FP8X4), rhs_scale=w3s[:, 0, b * KP:(b + 1) * KP], start=True, stop=True)
             sh[u] = held([P, PACK, P], F32, f"sh{u}")
             nc.scalar.copy(out=sh[u][:], in_=planes(bank))
 
         def turn_shift(u):
-            xt[u] = psum.tile([P, PACK, JC], F32, name=f"xt{u}", tag=f"xt{u % 4}")
+            xt[u] = psum.tile([P, PACK, JC], F32, name=f"xt{u}", tag=f"xt{(u + 2 * (u // CHUNKS)) % 4}")
             for t in range(PACK):
                 nc.tensor.matmul(xt[u][:, t, :], sh[u][:, t, :], ident[:], start=(t == 0), stop=False, is_transpose=True)
 
-        def do_motion(u):
+        def do_motion(u, passes=(0, 1)):
             b, c = units[u]
-            bank = product_bank([P, KP])
-            mo[u] = bank
-            for a in range(2):
+            if u not in mo:
+                mo[u] = product_bank([P, KP], c)
+            bank = mo[u]
+            first = 1 if u in (2, 3) else 0
+            for a in passes:
                 words = vw0[:, cols(c)] if a == 0 else vw1[c // 2][:, cols(c % 2)]
                 nc.tensor.matmul_mx(out=bank[:], lhsT=words.bitcast(FP8X4), lhsT_scale=vs[a][:, cols(c)],
                                     rhs=w1c[b][:, a, :].bitcast(FP4X4), rhs_scale=w1s[:, a, b * KP:(b + 1) * KP],
-                                    start=(a == 0), stop=(a == 1))
+                                    start=(a == first), stop=(a != first))
 
         def do_mul(u):
             bank = mo[u]
-            aa = held([P, PACK, P], F32, f"aa{u}")
+            aa = held([P, PACK, P], F32, f"aa{u}") if u != 3 else shared.tile([P, PACK, P], F32, name="aa3", offset=16384)
             for ts in ([slice(0, 2), slice(2, 4)] if u == len(units) - 1 else [slice(0, PACK)]):
                 nc.vector.scalar_tensor_tensor(out=aa[:, ts], in0=th[u][:, ts], scalar=1.0, in1=planes(bank)[:, ts],
                                                op0=ALU.add, op1=ALU.mult)
@@ -181,7 +179,7 @@ def tile_list_gait_breed_grading_kernel(tc, tab_words, tab_scales, tab2_words, t
             return [slice(0, JC // 2), slice(JC // 2, JC)] if u == len(units) - 1 else [slice(0, JC)]
 
         def do_silu(u):
-            ss[u] = held([P, JC, PACK], F32, f"ss{u}")
+            ss[u] = held([P, JC, PACK], F32, f"ss{u}", None if u else "tabs")
             for js in parts(u):
                 nc.scalar.activation(out=ss[u][:, js], in_=xt[u][:].rearrange("p t j -> p j t")[:, js], func=ACT.Silu)
 
@@ -189,11 +187,13 @@ def tile_list_gait_breed_grading_kernel(tc, tab_words, tab_scales, tab2_words, t
             b, c = units[u]
             for lo, hi in groups:
                 if u == lo:
-                    hw[lo] = held([P, (hi - lo) * JC, PACK], BF16, f"hb{lo}")
+                    shape = [P, (hi - lo) * JC, PACK]
+                    hw[lo] = held(shape, BF16, f"hb{lo}") if lo else shared.tile(shape, BF16, name="hb0", offset=18432, align_bytes=64)
                 if lo <= u < hi:
                     hb[u] = hw[lo][:, (u - lo) * JC:(u - lo + 1) * JC, :]
             for js in parts(u):
-                nc.vector.tensor_tensor(out=hb[u][:, js], in0=ss[u][:, js],
+                eng = nc.gpsimd if u in (0, 1, 2) else nc.vector
+                eng.tensor_tensor(out=hb[u][:, js], in0=ss[u][:, js],
                                         in1=gains[:, b, :].unsqueeze(1).to_broadcast([P, js.stop - js.start, PACK]), op=ALU.mult)
 
         def do_quant(lo, hi):
@@ -208,9 +208,6 @@ def tile_list_gait_breed_grading_kernel(tc, tab_words, tab_scales, tab2_words, t
         w4c = held([P, HALVES * N], U32, "w4c")
 
         def prepare_w4():
-            w4g = held([P, HALVES, N, PACK], BF16, "w4g", "aa4")
-            for b in range(HALVES):
-                weave(nc.scalar, w4g[:, b], w4raw[b][:])
             nc.vector.quantize_mx(out=w4c[:].bitcast(FP8X4), scales=w4s[:], in_=w4g[:].rearrange("p b n t -> p (b n t)"))
 
         def do_last_out(c):
@@ -246,58 +243,75 @@ def tile_list_gait_breed_grading_kernel(tc, tab_words, tab_scales, tab2_words, t
         round_w2(0, 0, nc.scalar)
         round_w2(0, 1, nc.vector)
         quantise_w2(0)
-        for u in range(CHUNKS):
+        for u in range(2 * CHUNKS):
             do_shift(u)
-            turn_shift(u)
         for u in range(CHUNKS):
             do_tanh(u)
-        vw0 = held([P, S], U32, "vw0", "w2g0")
+        vs[0] = held([P, S], U8, "vs0", "w2g0")
+        nc.vector.tensor_copy(out=vs[0][:], in_=tabs[:].indirect(list1[:]))
+        for r in range(4):
+            nc.sync.dma_start(out=vs[1][r:P:32].bitcast(I32), in_=vs[0][16 + r:P:32].bitcast(I32))
+        w2second = held([P, PACK, KP], F32, "w2second", "tabs")
+        load_w2(w2second, KP)
+        vw0 = held([P, S], U32, "vw0", "w2first1")
         nc.vector.tensor_copy(out=vw0[:], in_=tabw[0][:].indirect(list1[:]))
-        for a in range(2):
-            nc.vector.tensor_copy(out=vs[a][:], in_=tabs[:, a, :].indirect(list1[:]))
-        vw1[0] = held([P, S // 2], U32, "vw10")
-        nc.vector.tensor_copy(out=vw1[0][:], in_=tabw[1][:].indirect(list1[:, 0:16]))
+        w1c[1] = shared.tile([P, 2, KP // 2], I32, name="w1c1", offset=0, align_bytes=64)
+        load_w1(1)
+        w4raw = [shared.tile([P, PACK, N], F32, name=f"w4raw{b}", offset=2048 + 4096 * b) for b in range(HALVES)]
+        for b in range(HALVES):
+            nc.sync.dma_start(out=w4raw[b][:], in_=w4[b * KP:(b + 1) * KP, :].rearrange("(p t) n -> p t n", t=PACK))
         mo = {}
         for u in range(CHUNKS):
-            do_motion(u)
-            if u % 2 == 1:
-                do_shift(u + 3)
-                do_shift(u + 4)
-            do_mul(u)
-            if u == 0:
-                vw1[1] = held([P, S // 2], U32, "vw11")
-                nc.vector.tensor_copy(out=vw1[1][:], in_=tabw[1][:].indirect(list1[:, 16:32]))
-                do_silu(0)
-                w2g[1] = held([P, KP, PACK], BF16, "w2g1", "aa0")
-                round_w2(1, 0, nc.scalar)
+            turn_shift(u)
+        do_motion(0, (0,))
+        do_motion(1, (0,))
+        for h in range(2):
+            vw1[h] = held([P, S // 2], U32, f"vw1{h}")
+            nc.vector.tensor_copy(out=vw1[h][:], in_=tabw[1][:].indirect(list1[:, 16 * h:16 * h + 16]))
+        do_motion(0, (1,))
+        do_motion(1, (1,))
+        do_motion(2, (1, 0))
+        do_motion(3, (1, 0))
+        do_mul(0)
+        w2g[1] = shared.tile([P, KP, PACK], BF16, name="w2g1", offset=16384, align_bytes=64)
+        round_w2(1, 0, nc.scalar)
+        do_mul(1)
         round_w2(1, 1, nc.vector)
+        do_mul(2)
         quantise_w2(1)
+        do_mul(3)
+        do_silu(0)
         do_silu(1)
         do_silu(2)
-        do_tanh(4)
-        do_silu(3)
+        for u in range(CHUNKS, 2 * CHUNKS):
+            do_tanh(u)
+        for u in range(CHUNKS, 2 * CHUNKS):
+            do_motion(u)
         do_gain(0)
-        do_gain(1)
+        do_silu(3)
         for u in range(CHUNKS, 2 * CHUNKS):
             turn_shift(u)
-            if u + 1 < 2 * CHUNKS:
-                do_tanh(u + 1)
-            if u > CHUNKS:
-                do_silu(u - 1)
-            do_motion(u)
             do_mul(u)
-            do_gain(u - 2)
-            if u == 5:
-                do_quant(0, 4)
-            if u == 6:
-                prepare_w4()
+        w4g = held([P, HALVES, N, PACK], BF16, "w4g", "th5")
+        do_gain(1)
+        do_gain(2)
+        do_gain(3)
+        weave(nc.vector, w4g[:, 0], w4raw[0][:])
+        do_silu(4)
+        weave(nc.scalar, w4g[:, 1], w4raw[1][:])
+        do_silu(5)
+        do_silu(6)
         do_silu(7)
+        do_gain(4)
+        do_quant(0, 4)
+        prepare_w4()
+        do_gain(5)
         do_quant(4, 6)
+        do_gain(6)
         do_out(0)
         do_out(1)
-        do_gain(6)
         do_quant(6, 7)
-        do_out(2)
         do_gain(7)
+        do_out(2)
         do_quant(7, 8)
         do_last_out(3)

@@ -23,6 +23,7 @@ KP = P * PACK
 JC = 128
 CHUNKS = S // JC
 HALVES = H // KP
+QW = KP // 2
 
 
 def tile_list_gait_breed_grading_kernel(tc, tab_words, tab_scales, tab2_words, tab2_scales, offs, offs2,
@@ -32,30 +33,29 @@ def tile_list_gait_breed_grading_kernel(tc, tab_words, tab_scales, tab2_words, t
         keep = ctx.enter_context(tc.tile_pool(name="keep", bufs=1))
         shared = ctx.enter_context(tc.tile_pool(name="shared", bufs=1))
         psum = ctx.enter_context(tc.psum_pool(name="psum", bufs=1))
-        taken = []
 
-        def product_bank(shape, which=None):
-            taken.append(shape)
-            return psum.tile(shape, F32, name=f"prod{len(taken)}", tag=f"prod{len(taken) % 4 if which is None else which}")
+        def bank_tile(shape, name, bank):
+            return psum.tile(shape, F32, name=name, tag=f"bank{bank}")
 
         def held(shape, dtype, name, tag=None):
+            if isinstance(tag, int):
+                return shared.tile(shape, dtype, name=name, offset=tag, align_bytes=64)
             return keep.tile(shape, dtype, name=name, tag=tag or name, align_bytes=64)
 
         list1 = held([P, S // 16], U16, "list1")
         list2 = held([P, S // 16], U16, "list2")
         tab2w = held([P, T2], U16, "tab2w")
         tab2s = held([P, 1, T2], U8, "tab2s")
-        tabw = [shared.tile([P, T], U32, name="tabw0", offset=0), held([P, T], U32, "tabw1")]
-        tabs = held([P, T], U8, "tabs")
+        tabw = [held([P, T], U32, "tabw0"), held([P, T], U32, "tabw1")]
+        tabs = held([P, T], U8, "tabs", 8128)
         vs = {1: held([P, S], U8, "vs1")}
         w1s = held([P, 2, H], U8, "w1s")
         w3s = held([P, 1, H], U8, "w3s")
         warm = held([P, 2], F32, "warm")
         ident = held([P, P], F32, "ident")
         gains = held([P, HALVES, PACK], F32, "gains")
-        w2first = [held([P, PACK, KP // 2], F32, f"w2first{q}") for q in range(2)]
-        w1c = {0: held([P, 2, KP // 2], I32, "w1c0")}
         w3c = held([P, H], I32, "w3c")
+        w2raw, w1c, w1p, w4raw = {}, {}, {}, {}
 
         nc.vector.memset(tab2s[:, 0, :].bitcast(I32), 0)
         nc.vector.memset(warm[:, 0:1], 0.0)
@@ -65,48 +65,79 @@ def tile_list_gait_breed_grading_kernel(tc, tab_words, tab_scales, tab2_words, t
         nc.vector.memset(w1s[:].rearrange("p a n -> p (a n)").bitcast(I32), 0)
         nc.vector.memset(vs[1][:].bitcast(I32), 0)
 
-        def load_w2(tile, first):
-            width = tile.shape[2]
-            nc.sync.dma_start(out=tile[:], in_=w2[:, first:first + width].rearrange("(p j) c -> p j c", j=PACK))
+        def load_w2(q, tag=None):
+            w2raw[q] = held([P, PACK, QW], F32, f"w2raw{q}", tag)
+            nc.sync.dma_start(out=w2raw[q][:], in_=w2[:, q * QW:(q + 1) * QW].rearrange("(p j) c -> p j c", j=PACK))
 
+        def load_w2_half(b, tag=None):
+            both = held([P, PACK, KP], F32, f"w2half{b}", tag)
+            nc.sync.dma_start(out=both[:], in_=w2[:, b * KP:(b + 1) * KP].rearrange("(p j) c -> p j c", j=PACK))
+            w2raw[2 * b] = both[:, :, 0:QW]
+            w2raw[2 * b + 1] = both[:, :, QW:KP]
 
-        def load_w1(b):
+        def load_w2_rows(pair):
+            if not w2raw:
+                whole = held([P, PACK, H], F32, "w2whole")
+                w2raw["whole"] = whole
+                for q in range(H // QW):
+                    w2raw[q] = whole[:, :, q * QW:(q + 1) * QW]
+            rows = slice(2 * pair, 2 * pair + 2)
+            nc.sync.dma_start(out=w2raw["whole"][:, rows, :], in_=w2.rearrange("(p j) c -> p j c", j=PACK)[:, rows, :])
+
+        def load_w1_pass(a, tag=None):
+            w1p[a] = held([P, H // 2], I32, f"w1p{a}", tag)
+            nc.sync.dma_start(out=w1p[a][:], in_=w1_words[a].bitcast(I32))
+
+        def load_w1(b, tag=None):
+            w1c[b] = held([P, 2, KP // 2], I32, f"w1c{b}", tag)
             nc.sync.dma_start(out=w1c[b][:],
                               in_=w1_words.rearrange("a p n -> p a n")[:, :, 2 * KP * b:2 * KP * (b + 1)].bitcast(I32))
+
+        def load_w4(b, tag=None):
+            if not w4raw:
+                both = held([P, HALVES, PACK, N], F32, "w4raw", tag)
+                for half in range(HALVES):
+                    w4raw[half] = both[:, half]
+            nc.sync.dma_start(out=w4raw[b], in_=w4[b * KP:(b + 1) * KP, :].rearrange("(p t) n -> p t n", t=PACK))
 
         def load_tab(a):
             nc.sync.dma_start(out=tabw[a][:].bitcast(I32), in_=tab_words[a].rearrange("p n t -> p (n t)").bitcast(I32))
 
-        def scale_rows(eng, plane, scales):
+        def scale_rows(plane, scales):
             for r in range(4):
                 rows = scales[:, r:16:4, :].rearrange("a q n -> q a n").bitcast(I32)
-                eng.dma_start(out=plane[r:P:32].bitcast(I32), in_=rows)
+                nc.sync.dma_start(out=plane[r:P:32].bitcast(I32), in_=rows)
 
-        nc.sync.dma_start(out=tab2w[:].bitcast(I32), in_=tab2_words[0].bitcast(I32))
-        nc.sync.dma_start(list2[:], offs2)
-        scale_rows(nc.sync, tab2s[:], tab2_scales)
-        nc.sync.dma_start(out=w3c[:], in_=w3_words[0].rearrange("p n t -> p (n t)").bitcast(I32))
-        load_w2(w2first[0], 0)
-        scale_rows(nc.sync, w3s[:], w3_scales)
-        load_w2(w2first[1], KP // 2)
-        nc.sync.dma_start(list1[:], offs)
-        for r in range(4):
-            nc.sync.dma_start(out=tabs[r:P:16].bitcast(I32), in_=tab_scales[:, r:16:4, :].rearrange("a q n -> q a n").bitcast(I32))
-        load_tab(0)
-        load_w1(0)
-        scale_rows(nc.sync, w1s[:], w1_scales)
-        load_tab(1)
-        nc.sync.dma_start(out=gains[:], in_=gain.rearrange("(b p t) -> p b t", p=P, t=PACK))
-        make_identity(nc, ident[:])
+        def load_tabs():
+            for r in range(4):
+                nc.sync.dma_start(out=tabs[r:P:16].bitcast(I32),
+                                  in_=tab_scales[:, r:16:4, :].rearrange("a q n -> q a n").bitcast(I32))
+
+        def load_tab2w():
+            nc.sync.dma_start(out=tab2w[:].bitcast(I32), in_=tab2_words[0].bitcast(I32))
+
+        def load_w3():
+            nc.sync.dma_start(out=w3c[:], in_=w3_words[0].rearrange("p n t -> p (n t)").bitcast(I32))
+
+        def load_gain():
+            nc.sync.dma_start(out=gains[:], in_=gain.rearrange("(b p t) -> p b t", p=P, t=PACK))
+
+        def move_rows():
+            for r in range(4):
+                nc.sync.dma_start(out=vs[1][r:P:32].bitcast(I32), in_=vs[0][16 + r:P:32].bitcast(I32))
 
         v2w = held([P, S], U16, "v2w")
         v2s = held([P, S], U8, "v2s")
-        vw1 = {}
+        vw = {}
 
         def cols(c):
             return slice(c * JC, (c + 1) * JC)
 
         def weave(eng, dst, raw):
+            if eng is nc.gpsimd:
+                nc.gpsimd.tensor_scalar(out=dst, in0=raw.rearrange("p t c -> p c t"), scalar1=1.0, scalar2=0.0,
+                                        op0=ALU.mult, op1=ALU.add)
+                return
             d = dst.rearrange("p (c i) t -> p c t i", i=4)
             s = raw.rearrange("p t (c i) -> p c t i", i=4)
             if eng is nc.scalar:
@@ -114,204 +145,322 @@ def tile_list_gait_breed_grading_kernel(tc, tab_words, tab_scales, tab2_words, t
             else:
                 nc.vector.tensor_copy(out=d, in_=s)
 
-        w2g = {}
+        w2g, w4g = {}, {}
         w2c = [held([P, KP], U32, f"w2c{b}") for b in range(HALVES)]
         w2s = [held([P, KP], U8, f"w2s{b}") for b in range(HALVES)]
 
-        def round_w2(b, q, eng):
-            half = slice(q * KP // 2, (q + 1) * KP // 2)
-            weave(eng, w2g[b][:, half], w2second[:, :, half] if b else w2first[q][:])
+        def round_w2(q, eng, tag=None, lo=0, hi=QW):
+            b = q // 2
+            if b not in w2g:
+                w2g[b] = held([P, KP, PACK], BF16, f"w2g{b}", tag)
+            first = (q % 2) * QW
+            weave(eng, w2g[b][:, first + lo:first + hi], w2raw[q][:, :, lo:hi])
 
         def quantise_w2(b):
             nc.vector.quantize_mx(out=w2c[b][:].bitcast(FP8X4), scales=w2s[b][:], in_=w2g[b][:].rearrange("p c t -> p (c t)"))
 
+        def gather_scales(tag=None):
+            vs[0] = held([P, S], U8, "vs0", tag)
+            nc.vector.tensor_copy(out=vs[0][:], in_=tabs[:].indirect(list1[:]))
+
+        def gather_words(a, lo, hi, tag=None):
+            tile = held([P, (hi - lo) * JC], U32, f"vw{a}{lo}", tag)
+            nc.vector.tensor_copy(out=tile[:], in_=tabw[a][:].indirect(list1[:, 8 * lo:8 * hi]))
+            for c in range(lo, hi):
+                vw[a, c] = tile[:, cols(c - lo)]
+
         units = [(b, c) for b in range(HALVES) for c in range(CHUNKS)]
-        th, sh, xt, ss, hb = {}, {}, {}, {}, {}
-        groups = [(0, 4), (4, 6), (6, 7), (7, 8)]
-        hc, hs, hw = {}, {}, {}
+        groups = [(0, 4), (4, 5), (5, 6), (6, 7), (7, 8)]
+        th, sh, xt, ss, hb, mo, aa, sc, sp = {}, {}, {}, {}, {}, {}, {}, {}, {}
+        hc, hs, hw, begun = {}, {}, {}, {}
 
         def planes(bank):
             return bank[:].rearrange("p (q t) -> p t q", t=PACK)
 
-        def do_tanh(u):
+        def do_scale(u, bank):
             b, c = units[u]
-            bank = psum.tile([P, KP], F32, name=f"scale{u}", tag=f"xt{u - 6}") if u >= 6 else product_bank([P, KP], c + 2 * b)
-            nc.tensor.matmul_mx(out=bank[:], lhsT=v2w[:, cols(c)].bitcast(FP4X4), lhsT_scale=v2s[:, cols(c)],
+            sc[u] = bank_tile([P, KP], f"scale{u}", bank)
+            nc.tensor.matmul_mx(out=sc[u][:], lhsT=v2w[:, cols(c)].bitcast(FP4X4), lhsT_scale=v2s[:, cols(c)],
                                 rhs=w2c[b][:].bitcast(FP8X4), rhs_scale=w2s[b][:], start=True, stop=True)
-            th[u] = held([P, PACK, P], F32, f"th{u}") if u else shared.tile([P, PACK, P], F32, name="th0", offset=16384)
-            nc.scalar.activation(out=th[u][:], in_=planes(bank), func=ACT.Tanh)
 
-        def do_shift(u):
+        def do_tanh(u, tag=None):
+            th[u] = held([P, PACK, P], F32, f"th{u}", tag)
+            nc.scalar.activation(out=th[u][:], in_=planes(sc[u]), func=ACT.Tanh)
+
+        def do_shift(u, bank):
             b, c = units[u]
-            bank = psum.tile([P, KP], F32, name=f"shift{u}", tag=f"xt{c}") if b else product_bank([P, KP], c)
-            nc.tensor.matmul_mx(out=bank[:], lhsT=v2w[:, cols(c)].bitcast(FP4X4), lhsT_scale=v2s[:, cols(c)],
-                                rhs=w3c[:, b * KP:(b + 1) * KP].bitcast(FP8X4), rhs_scale=w3s[:, 0, b * KP:(b + 1) * KP], start=True, stop=True)
-            sh[u] = held([P, PACK, P], F32, f"sh{u}")
-            nc.scalar.copy(out=sh[u][:], in_=planes(bank))
+            sp[u] = bank_tile([P, KP], f"shift{u}", bank)
+            nc.tensor.matmul_mx(out=sp[u][:], lhsT=v2w[:, cols(c)].bitcast(FP4X4), lhsT_scale=v2s[:, cols(c)],
+                                rhs=w3c[:, b * KP:(b + 1) * KP].bitcast(FP8X4), rhs_scale=w3s[:, 0, b * KP:(b + 1) * KP],
+                                start=True, stop=True)
 
-        def turn_shift(u):
-            xt[u] = psum.tile([P, PACK, JC], F32, name=f"xt{u}", tag=f"xt{(u + 2 * (u // CHUNKS)) % 4}")
+        def copy_shift(u, eng, tag=None):
+            sh[u] = held([P, PACK, P], F32, f"sh{u}", tag)
+            if eng is nc.scalar:
+                nc.scalar.copy(out=sh[u][:], in_=planes(sp[u]))
+            else:
+                nc.vector.tensor_copy(out=sh[u][:], in_=planes(sp[u]))
+
+        def turn(u, src, bank, last):
+            opens = u not in xt
+            if opens:
+                xt[u] = bank_tile([P, PACK, JC], f"xt{u}", bank)
             for t in range(PACK):
-                nc.tensor.matmul(xt[u][:, t, :], sh[u][:, t, :], ident[:], start=(t == 0), stop=False, is_transpose=True)
+                nc.tensor.matmul(xt[u][:, t, :], src[:, t, :], ident[:], start=(opens and t == 0),
+                                 stop=(last and t == PACK - 1), is_transpose=True)
 
-        def do_motion(u, passes=(0, 1)):
+        def do_motion(u, passes, bank=None):
             b, c = units[u]
             if u not in mo:
-                mo[u] = product_bank([P, KP], c)
-            bank = mo[u]
-            first = 1 if u in (2, 3) else 0
+                mo[u] = bank_tile([P, KP], f"motion{u}", bank)
             for a in passes:
-                words = vw0[:, cols(c)] if a == 0 else vw1[c // 2][:, cols(c % 2)]
-                nc.tensor.matmul_mx(out=bank[:], lhsT=words.bitcast(FP8X4), lhsT_scale=vs[a][:, cols(c)],
-                                    rhs=w1c[b][:, a, :].bitcast(FP4X4), rhs_scale=w1s[:, a, b * KP:(b + 1) * KP],
-                                    start=(a == first), stop=(a != first))
+                nc.tensor.matmul_mx(out=mo[u][:], lhsT=vw[a, c].bitcast(FP8X4), lhsT_scale=vs[a][:, cols(c)],
+                                    rhs=(w1p[a][:, b * QW:(b + 1) * QW] if w1p else w1c[b][:, a, :]).bitcast(FP4X4), rhs_scale=w1s[:, a, b * KP:(b + 1) * KP],
+                                    start=(u not in begun), stop=(u in begun))
+                begun[u] = True
 
-        def do_mul(u):
-            bank = mo[u]
-            aa = held([P, PACK, P], F32, f"aa{u}") if u != 3 else shared.tile([P, PACK, P], F32, name="aa3", offset=16384)
+        def do_mul(u, tag=None):
+            aa[u] = held([P, PACK, P], F32, f"aa{u}", tag)
             for ts in ([slice(0, 2), slice(2, 4)] if u == len(units) - 1 else [slice(0, PACK)]):
-                nc.vector.scalar_tensor_tensor(out=aa[:, ts], in0=th[u][:, ts], scalar=1.0, in1=planes(bank)[:, ts],
+                nc.vector.scalar_tensor_tensor(out=aa[u][:, ts], in0=th[u][:, ts], scalar=1.0, in1=planes(mo[u])[:, ts],
                                                op0=ALU.add, op1=ALU.mult)
-            for t in range(PACK):
-                nc.tensor.matmul(xt[u][:, t, :], aa[:, t, :], ident[:], start=False, stop=(t == PACK - 1), is_transpose=True)
 
         def parts(u):
             return [slice(0, JC // 2), slice(JC // 2, JC)] if u == len(units) - 1 else [slice(0, JC)]
 
-        def do_silu(u):
-            ss[u] = held([P, JC, PACK], F32, f"ss{u}", None if u else "tabs")
+        def do_silu(u, tag=None):
+            ss[u] = held([P, JC, PACK], F32, f"ss{u}", tag)
             for js in parts(u):
                 nc.scalar.activation(out=ss[u][:, js], in_=xt[u][:].rearrange("p t j -> p j t")[:, js], func=ACT.Silu)
 
-        def do_gain(u):
+        def do_gain(u, eng, tag=None):
             b, c = units[u]
             for lo, hi in groups:
-                if u == lo:
-                    shape = [P, (hi - lo) * JC, PACK]
-                    hw[lo] = held(shape, BF16, f"hb{lo}") if lo else shared.tile(shape, BF16, name="hb0", offset=18432, align_bytes=64)
                 if lo <= u < hi:
+                    if lo not in hw:
+                        hw[lo] = held([P, (hi - lo) * JC, PACK], BF16, f"hb{lo}", tag)
                     hb[u] = hw[lo][:, (u - lo) * JC:(u - lo + 1) * JC, :]
             for js in parts(u):
-                eng = nc.gpsimd if u in (0, 1, 2) else nc.vector
                 eng.tensor_tensor(out=hb[u][:, js], in0=ss[u][:, js],
-                                        in1=gains[:, b, :].unsqueeze(1).to_broadcast([P, js.stop - js.start, PACK]), op=ALU.mult)
+                                  in1=gains[:, b, :].unsqueeze(1).to_broadcast([P, js.stop - js.start, PACK]), op=ALU.mult)
 
-        def do_quant(lo, hi):
-            codes = held([P, (hi - lo) * JC], U32, f"hc{lo}")
+        gain_rows = held([P, P], F32, "gain_rows")
+        gain_bank = {}
+
+        def load_gain_rows():
+            nc.vector.memset(gain_rows[:], 0.0)
+            with nc.allow_non_contiguous_dma(reason="one gain value an element"):
+                for b in range(HALVES):
+                    nc.sync.dma_start(out=gain_rows[PACK * b:PACK * (b + 1), :],
+                                      in_=gain[b * KP:(b + 1) * KP].rearrange("(p t) -> t p", t=PACK))
+
+        def turn_gain(bank):
+            gain_bank[0] = bank_tile([P, P], "gain_bank", bank)
+            nc.tensor.matmul(gain_bank[0][:], gain_rows[:], ident[:], start=True, stop=True, is_transpose=True)
+
+        def gain_from_bank(u, tag=None):
+            b, c = units[u]
+            dst = group_tile(u, tag)
+            for js in parts(u):
+                factor = gain_bank[0][:, PACK * b:PACK * (b + 1)].unsqueeze(1).to_broadcast([P, js.stop - js.start, PACK])
+                nc.vector.tensor_tensor(out=dst[:, js], in0=ss[u][:, js], in1=factor, op=ALU.mult)
+
+        def group_tile(u, tag=None):
+            for lo, hi in groups:
+                if lo <= u < hi:
+                    if lo not in hw:
+                        hw[lo] = held([P, (hi - lo) * JC, PACK], BF16, f"hb{lo}", tag)
+                    return hw[lo][:, (u - lo) * JC:(u - lo + 1) * JC, :]
+
+        def silu_planes(u, tag=None):
+            ss[u] = held([P, PACK, JC], F32, f"ss{u}", tag)
+            nc.scalar.activation(out=ss[u][:], in_=xt[u][:], func=ACT.Silu)
+
+        def gain_planes(u, tag=None):
+            b, c = units[u]
+            hb[u] = held([P, PACK, JC], BF16, f"hp{u}", tag)
+            for t in range(PACK):
+                nc.scalar.activation(out=hb[u][:, t, :], in_=ss[u][:, t, :], func=ACT.Copy, scale=gains[:, b, t:t + 1])
+
+        def weave_h(u, tag=None):
+            weave(nc.vector, group_tile(u, tag), hb[u][:])
+
+        def do_quant(lo, tag=None):
+            hi = dict(groups)[lo]
+            codes = held([P, (hi - lo) * JC], U32, f"hc{lo}", tag)
             plane = held([P, (hi - lo) * JC], U8, f"hs{lo}")
             for u in range(lo, hi):
-                hc[u] = codes[:, (u - lo) * JC:(u - lo + 1) * JC]
-                hs[u] = plane[:, (u - lo) * JC:(u - lo + 1) * JC]
+                hc[units[u]] = (codes, (u - lo) * JC)
+                hs[units[u]] = plane
             nc.vector.quantize_mx(out=codes[:].bitcast(FP8X4), scales=plane[:], in_=hw[lo][:].rearrange("p j t -> p (j t)"))
 
-        w4s = held([P, HALVES * N], U8, "w4s")
-        w4c = held([P, HALVES * N], U32, "w4c")
+        w4s, w4c = {}, {}
 
-        def prepare_w4():
-            nc.vector.quantize_mx(out=w4c[:].bitcast(FP8X4), scales=w4s[:], in_=w4g[:].rearrange("p b n t -> p (b n t)"))
+        def round_w4(b, eng, tag=None):
+            w4g[b] = held([P, N, PACK], BF16, f"w4g{b}", tag)
+            weave(eng, w4g[b][:], w4raw[b])
 
-        def do_last_out(c):
-            banks = [product_bank([P, JC]), psum.tile([P, JC], F32, name="last", tag="xt0")]
+        def quantise_w4(b, tag=None):
+            w4c[b] = held([P, N], U32, f"w4c{b}", tag)
+            w4s[b] = held([P, N], U8, f"w4s{b}")
+            nc.vector.quantize_mx(out=w4c[b][:].bitcast(FP8X4), scales=w4s[b][:], in_=w4g[b][:].rearrange("p n t -> p (n t)"))
+
+        def out_pass(dst, b, h, c, width, start, stop):
+            codes, first = hc[b, c]
+            nc.tensor.matmul_mx(out=dst, lhsT=w4c[b][:, h * P:(h + 1) * P].bitcast(FP8X4), lhsT_scale=w4s[b][:, h * P:(h + 1) * P],
+                                rhs=codes[:, first:first + width].bitcast(FP8X4), rhs_scale=hs[b, c][:, first:first + width],
+                                start=start, stop=stop)
+
+        def do_last_out(c, bank0, bank1):
+            banks = [bank_tile([P, JC], "last0", bank0), bank_tile([P, JC], "last1", bank1)]
             for b in range(HALVES):
                 for h in range(N // P):
-                    u = b * CHUNKS + c
-                    w = slice(b * N + h * P, b * N + (h + 1) * P)
-                    nc.tensor.matmul_mx(out=banks[h][:], lhsT=w4c[:, w].bitcast(FP8X4), lhsT_scale=w4s[:, w],
-                                        rhs=hc[u].bitcast(FP8X4), rhs_scale=hs[u], start=(b == 0), stop=(b == HALVES - 1))
+                    out_pass(banks[h][:], b, h, c, JC, b == 0, b == HALVES - 1)
             res = [held([P, JC], F32, f"last{h}") for h in range(N // P)]
             nc.vector.tensor_copy(out=res[0][:], in_=banks[0][:])
             nc.sync.dma_start(out=out[0:P, cols(c)], in_=res[0][:])
             nc.scalar.copy(out=res[1][:], in_=banks[1][:])
             nc.scalar.dma_start(out=out[P:2 * P, cols(c)], in_=res[1][:])
 
-        def do_out(c):
-            bank = product_bank([P, N // P, JC])
+        def do_out(c, chunks, bank, eng):
+            width = chunks * JC
+            acc = bank_tile([P, N // P, width], f"out{c}", bank)
             for b in range(HALVES):
                 for h in range(N // P):
-                    u = b * CHUNKS + c
-                    w = slice(b * N + h * P, b * N + (h + 1) * P)
-                    nc.tensor.matmul_mx(out=bank[:, h, :], lhsT=w4c[:, w].bitcast(FP8X4), lhsT_scale=w4s[:, w],
-                                        rhs=hc[u].bitcast(FP8X4), rhs_scale=hs[u], start=(b == 0 and h == 0),
-                                        stop=(b == HALVES - 1 and h == N // P - 1))
-            res = held([P, N // P, JC], F32, f"res{c}")
-            nc.scalar.copy(out=res[:], in_=bank[:])
-            nc.sync.dma_start(out=out.rearrange("(h p) j -> p h j", p=P)[:, :, cols(c)], in_=res[:])
+                    out_pass(acc[:, h, :], b, h, c, width, b == 0 and h == 0, b == HALVES - 1 and h == N // P - 1)
+            res = held([P, N // P, width], F32, f"res{c}")
+            if eng is nc.scalar:
+                nc.scalar.copy(out=res[:], in_=acc[:])
+            else:
+                nc.vector.tensor_copy(out=res[:], in_=acc[:])
+            nc.sync.dma_start(out=out.rearrange("(h p) j -> p h j", p=P)[:, :, c * JC:c * JC + width], in_=res[:])
 
+        load_tab2w()
+        nc.sync.dma_start(list2[:], offs2)
+        load_w3()
+        scale_rows(tab2s[:], tab2_scales)
+        load_w2(0)
+        scale_rows(w3s[:], w3_scales)
+        load_w2(1)
+        nc.sync.dma_start(list1[:], offs)
+        load_w2_half(1)
+        load_tabs()
+        load_tab(0)
+        load_w1_pass(0)
+        scale_rows(w1s[:], w1_scales)
+        load_tab(1)
+        make_identity(nc, ident[:])
         nc.vector.tensor_copy(out=v2w[:], in_=tab2w[:].indirect(list2[:]))
         nc.vector.tensor_copy(out=v2s[:], in_=tab2s[:, 0, :].indirect(list2[:]))
-        w2g[0] = held([P, KP, PACK], BF16, "w2g0")
-        round_w2(0, 0, nc.scalar)
-        round_w2(0, 1, nc.vector)
+        round_w2(0, nc.vector)
+        round_w2(1, nc.vector)
         quantise_w2(0)
-        for u in range(2 * CHUNKS):
-            do_shift(u)
-        for u in range(CHUNKS):
-            do_tanh(u)
-        vs[0] = held([P, S], U8, "vs0", "w2g0")
-        nc.vector.tensor_copy(out=vs[0][:], in_=tabs[:].indirect(list1[:]))
-        for r in range(4):
-            nc.sync.dma_start(out=vs[1][r:P:32].bitcast(I32), in_=vs[0][16 + r:P:32].bitcast(I32))
-        w2second = held([P, PACK, KP], F32, "w2second", "tabs")
-        load_w2(w2second, KP)
-        vw0 = held([P, S], U32, "vw0", "w2first1")
-        nc.vector.tensor_copy(out=vw0[:], in_=tabw[0][:].indirect(list1[:]))
-        w1c[1] = shared.tile([P, 2, KP // 2], I32, name="w1c1", offset=0, align_bytes=64)
-        load_w1(1)
-        w4raw = [shared.tile([P, PACK, N], F32, name=f"w4raw{b}", offset=2048 + 4096 * b) for b in range(HALVES)]
-        for b in range(HALVES):
-            nc.sync.dma_start(out=w4raw[b][:], in_=w4[b * KP:(b + 1) * KP, :].rearrange("(p t) n -> p t n", t=PACK))
-        mo = {}
-        for u in range(CHUNKS):
-            turn_shift(u)
-        do_motion(0, (0,))
-        do_motion(1, (0,))
-        for h in range(2):
-            vw1[h] = held([P, S // 2], U32, f"vw1{h}")
-            nc.vector.tensor_copy(out=vw1[h][:], in_=tabw[1][:].indirect(list1[:, 16 * h:16 * h + 16]))
+        do_shift(0, 0)
+        do_shift(1, 1)
+        do_shift(2, 2)
+        do_shift(3, 3)
+        do_shift(4, 4)
+        do_shift(5, 5)
+        do_shift(6, 6)
+        do_shift(7, 7)
+        copy_shift(0, nc.scalar)
+        copy_shift(1, nc.scalar)
+        copy_shift(2, nc.scalar)
+        copy_shift(3, nc.scalar)
+        copy_shift(4, nc.scalar)
+        copy_shift(5, nc.scalar)
+        copy_shift(6, nc.scalar)
+        copy_shift(7, nc.scalar)
+        do_scale(0, 0)
+        do_scale(1, 1)
+        do_scale(2, 2)
+        do_scale(3, 3)
+        do_tanh(0)
+        do_tanh(1)
+        do_tanh(2)
+        do_tanh(3)
+        turn(0, sh[0], 4, False)
+        turn(1, sh[1], 5, False)
+        turn(2, sh[2], 6, False)
+        turn(3, sh[3], 7, False)
+        round_w2(2, nc.vector)
+        round_w2(3, nc.vector)
+        quantise_w2(1)
+        gather_scales("w2g1")
+        move_rows()
+        load_w1_pass(1, 10112)
+        load_gain()
+        load_w4(0, 0)
+        load_w4(1)
+        do_scale(4, 0)
+        do_scale(5, 1)
+        do_scale(6, 2)
+        do_scale(7, 3)
+        do_tanh(4)
+        do_tanh(5)
+        do_tanh(6)
+        do_tanh(7)
+        gather_words(0, 0, 4, "w2g0")
+        do_motion(0, (0,), 0)
+        do_motion(1, (0,), 1)
+        do_motion(2, (0,), 2)
+        do_motion(3, (0,), 3)
+        gather_words(1, 0, 2)
+        gather_words(1, 2, 4)
         do_motion(0, (1,))
         do_motion(1, (1,))
-        do_motion(2, (1, 0))
-        do_motion(3, (1, 0))
+        do_motion(2, (1,))
+        do_motion(3, (1,))
         do_mul(0)
-        w2g[1] = shared.tile([P, KP, PACK], BF16, name="w2g1", offset=16384, align_bytes=64)
-        round_w2(1, 0, nc.scalar)
         do_mul(1)
-        round_w2(1, 1, nc.vector)
         do_mul(2)
-        quantise_w2(1)
         do_mul(3)
+        do_motion(4, (0, 1,), 0)
+        turn(0, aa[0], None, True)
+        turn(1, aa[1], None, True)
+        round_w4(0, nc.scalar)
         do_silu(0)
         do_silu(1)
+        do_motion(5, (0, 1,), 1)
+        do_mul(4)
+        quantise_w4(0)
+        do_gain(0, nc.gpsimd)
+        do_mul(5)
+        turn(2, aa[2], None, True)
+        turn(4, sh[4], 2, False)
+        turn(3, aa[3], None, True)
         do_silu(2)
-        for u in range(CHUNKS, 2 * CHUNKS):
-            do_tanh(u)
-        for u in range(CHUNKS, 2 * CHUNKS):
-            do_motion(u)
-        do_gain(0)
         do_silu(3)
-        for u in range(CHUNKS, 2 * CHUNKS):
-            turn_shift(u)
-            do_mul(u)
-        w4g = held([P, HALVES, N, PACK], BF16, "w4g", "th5")
-        do_gain(1)
-        do_gain(2)
-        do_gain(3)
-        weave(nc.vector, w4g[:, 0], w4raw[0][:])
+        round_w4(1, nc.scalar, "aa3")
+        do_gain(1, nc.vector)
+        do_gain(2, nc.vector)
+        do_motion(6, (0, 1,), 0)
+        do_motion(7, (0, 1,), 1)
+        do_gain(3, nc.gpsimd)
+        do_mul(6)
+        do_mul(7)
+        turn(4, aa[4], None, True)
+        turn(5, sh[5], 3, False)
+        turn(5, aa[5], None, True)
+        turn(6, sh[6], 4, False)
+        turn(6, aa[6], None, True)
+        turn(7, sh[7], 5, False)
+        turn(7, aa[7], None, True)
         do_silu(4)
-        weave(nc.scalar, w4g[:, 1], w4raw[1][:])
         do_silu(5)
         do_silu(6)
         do_silu(7)
-        do_gain(4)
-        do_quant(0, 4)
-        prepare_w4()
-        do_gain(5)
-        do_quant(4, 6)
-        do_gain(6)
-        do_out(0)
-        do_out(1)
-        do_quant(6, 7)
-        do_gain(7)
-        do_out(2)
-        do_quant(7, 8)
-        do_last_out(3)
+        quantise_w4(1)
+        do_quant(0)
+        do_gain(4, nc.vector)
+        do_gain(5, nc.vector)
+        do_quant(4)
+        do_gain(6, nc.vector)
+        do_quant(5)
+        do_out(0, 1, 6, nc.scalar)
+        do_quant(6)
+        do_out(1, 1, 7, nc.scalar)
+        do_gain(7, nc.vector)
+        do_out(2, 1, 2, nc.scalar)
+        do_quant(7)
+        do_last_out(3, 0, 1)

@@ -53,7 +53,7 @@ def tile_list_gait_breed_grading_kernel(tc, tab_words, tab_scales, tab2_words, t
         w3s = held([P, 1, H], U8, "w3s")
         warm = held([P, 2], F32, "warm")
         ident = held([P, P], F32, "ident")
-        gains = held([P, HALVES, PACK], F32, "gains")
+        gains = held([P, HALVES, PACK], F32, "gains", 9344)
         w3c = held([P, H], I32, "w3c")
         w2raw, w1c, w1p, w4raw = {}, {}, {}, {}
 
@@ -87,6 +87,12 @@ def tile_list_gait_breed_grading_kernel(tc, tab_words, tab_scales, tab2_words, t
         def load_w1_pass(a, tag=None):
             w1p[a] = held([P, H // 2], I32, f"w1p{a}", tag)
             nc.sync.dma_start(out=w1p[a][:], in_=w1_words[a].bitcast(I32))
+
+        w1q = {}
+
+        def load_w1_piece(a, b, tag=None):
+            w1q[a, b] = held([P, QW], I32, f"w1q{a}{b}", tag)
+            nc.sync.dma_start(out=w1q[a, b][:], in_=w1_words[a][:, 2 * KP * b:2 * KP * (b + 1)].bitcast(I32))
 
         def load_w1(b, tag=None):
             w1c[b] = held([P, 2, KP // 2], I32, f"w1c{b}", tag)
@@ -159,6 +165,37 @@ def tile_list_gait_breed_grading_kernel(tc, tab_words, tab_scales, tab2_words, t
         def quantise_w2(b):
             nc.vector.quantize_mx(out=w2c[b][:].bitcast(FP8X4), scales=w2s[b][:], in_=w2g[b][:].rearrange("p c t -> p (c t)"))
 
+        w2q = {}
+
+        def quantise_quarter(q):
+            w2q[q] = (held([P, QW], U32, f"w2qc{q}"), held([P, QW], U8, f"w2qs{q}"))
+            nc.vector.quantize_mx(out=w2q[q][0][:].bitcast(FP8X4), scales=w2q[q][1][:],
+                                  in_=w2r[q][:].rearrange("p c t -> p (c t)"))
+
+        w2r = {}
+
+        def round_quarter(q, eng, tag=None):
+            w2r[q] = held([P, QW, PACK], BF16, f"w2r{q}", tag)
+            weave(eng, w2r[q][:], w2raw[q][:])
+
+        pair_bank, pair_th = {}, {}
+
+        def scale_pair(u, q, bank):
+            pair_bank[u, q] = bank_tile([P, 2, QW], f"scale{u}q{q}", bank)
+            for i in range(2):
+                c = units[u + i][1]
+                nc.tensor.matmul_mx(out=pair_bank[u, q][:, i, :], lhsT=v2w[:, cols(c)].bitcast(FP4X4), lhsT_scale=v2s[:, cols(c)],
+                                    rhs=w2q[q][0][:].bitcast(FP8X4), rhs_scale=w2q[q][1][:], start=True, stop=True)
+
+        def tanh_pair(u, q):
+            if u not in pair_th:
+                pair_th[u] = held([P, 2, PACK, P], F32, f"thp{u}")
+                for i in range(2):
+                    th[u + i] = pair_th[u][:, i]
+            half = slice((q % 2) * P // 2, (q % 2 + 1) * P // 2)
+            nc.scalar.activation(out=pair_th[u][:, :, :, half], in_=pair_bank[u, q][:].rearrange("p i (q t) -> p i t q", t=PACK),
+                                 func=ACT.Tanh)
+
         def gather_scales(tag=None):
             vs[0] = held([P, S], U8, "vs0", tag)
             nc.vector.tensor_copy(out=vs[0][:], in_=tabs[:].indirect(list1[:]))
@@ -215,7 +252,7 @@ def tile_list_gait_breed_grading_kernel(tc, tab_words, tab_scales, tab2_words, t
                 mo[u] = bank_tile([P, KP], f"motion{u}", bank)
             for a in passes:
                 nc.tensor.matmul_mx(out=mo[u][:], lhsT=vw[a, c].bitcast(FP8X4), lhsT_scale=vs[a][:, cols(c)],
-                                    rhs=(w1p[a][:, b * QW:(b + 1) * QW] if w1p else w1c[b][:, a, :]).bitcast(FP4X4), rhs_scale=w1s[:, a, b * KP:(b + 1) * KP],
+                                    rhs=(w1c[b][:, a, :] if b else w1q[a, b][:]).bitcast(FP4X4), rhs_scale=w1s[:, a, b * KP:(b + 1) * KP],
                                     start=(u not in begun), stop=(u in begun))
                 begun[u] = True
 
@@ -224,6 +261,11 @@ def tile_list_gait_breed_grading_kernel(tc, tab_words, tab_scales, tab2_words, t
             for ts in ([slice(0, 2), slice(2, 4)] if u == len(units) - 1 else [slice(0, PACK)]):
                 nc.vector.scalar_tensor_tensor(out=aa[u][:, ts], in0=th[u][:, ts], scalar=1.0, in1=planes(mo[u])[:, ts],
                                                op0=ALU.add, op1=ALU.mult)
+
+        def add_shift(u, eng, tag=None):
+            total = held([P, PACK, P], F32, f"sum{u}", tag)
+            eng.tensor_tensor(out=total[:], in0=aa[u][:], in1=sh[u][:], op=ALU.add)
+            aa[u] = total
 
         def parts(u):
             return [slice(0, JC // 2), slice(JC // 2, JC)] if u == len(units) - 1 else [slice(0, JC)]
@@ -243,27 +285,6 @@ def tile_list_gait_breed_grading_kernel(tc, tab_words, tab_scales, tab2_words, t
             for js in parts(u):
                 eng.tensor_tensor(out=hb[u][:, js], in0=ss[u][:, js],
                                   in1=gains[:, b, :].unsqueeze(1).to_broadcast([P, js.stop - js.start, PACK]), op=ALU.mult)
-
-        gain_rows = held([P, P], F32, "gain_rows")
-        gain_bank = {}
-
-        def load_gain_rows():
-            nc.vector.memset(gain_rows[:], 0.0)
-            with nc.allow_non_contiguous_dma(reason="one gain value an element"):
-                for b in range(HALVES):
-                    nc.sync.dma_start(out=gain_rows[PACK * b:PACK * (b + 1), :],
-                                      in_=gain[b * KP:(b + 1) * KP].rearrange("(p t) -> t p", t=PACK))
-
-        def turn_gain(bank):
-            gain_bank[0] = bank_tile([P, P], "gain_bank", bank)
-            nc.tensor.matmul(gain_bank[0][:], gain_rows[:], ident[:], start=True, stop=True, is_transpose=True)
-
-        def gain_from_bank(u, tag=None):
-            b, c = units[u]
-            dst = group_tile(u, tag)
-            for js in parts(u):
-                factor = gain_bank[0][:, PACK * b:PACK * (b + 1)].unsqueeze(1).to_broadcast([P, js.stop - js.start, PACK])
-                nc.vector.tensor_tensor(out=dst[:, js], in0=ss[u][:, js], in1=factor, op=ALU.mult)
 
         def group_tile(u, tag=None):
             for lo, hi in groups:
@@ -337,18 +358,18 @@ def tile_list_gait_breed_grading_kernel(tc, tab_words, tab_scales, tab2_words, t
 
         load_tab2w()
         nc.sync.dma_start(list2[:], offs2)
-        load_w3()
         scale_rows(tab2s[:], tab2_scales)
-        load_w2(0)
+        load_w3()
+        load_w2_half(0)
         scale_rows(w3s[:], w3_scales)
-        load_w2(1)
         nc.sync.dma_start(list1[:], offs)
         load_w2_half(1)
         load_tabs()
         load_tab(0)
-        load_w1_pass(0)
+        load_w1_piece(0, 0)
         scale_rows(w1s[:], w1_scales)
         load_tab(1)
+        load_w1_piece(1, 0)
         make_identity(nc, ident[:])
         nc.vector.tensor_copy(out=v2w[:], in_=tab2w[:].indirect(list2[:]))
         nc.vector.tensor_copy(out=v2s[:], in_=tab2s[:, 0, :].indirect(list2[:]))
@@ -388,9 +409,9 @@ def tile_list_gait_breed_grading_kernel(tc, tab_words, tab_scales, tab2_words, t
         quantise_w2(1)
         gather_scales("w2g1")
         move_rows()
-        load_w1_pass(1, 10112)
-        load_gain()
+        load_w1(1, 10112)
         load_w4(0, 0)
+        load_gain()
         load_w4(1)
         do_scale(4, 0)
         do_scale(5, 1)
@@ -423,25 +444,25 @@ def tile_list_gait_breed_grading_kernel(tc, tab_words, tab_scales, tab2_words, t
         do_silu(1)
         do_motion(5, (0, 1,), 1)
         do_mul(4)
+        add_shift(4, nc.vector)
         quantise_w4(0)
         do_gain(0, nc.gpsimd)
         do_mul(5)
         turn(2, aa[2], None, True)
-        turn(4, sh[4], 2, False)
         turn(3, aa[3], None, True)
         do_silu(2)
         do_silu(3)
         round_w4(1, nc.scalar, "aa3")
+        add_shift(5, nc.vector)
         do_gain(1, nc.vector)
         do_gain(2, nc.vector)
-        do_motion(6, (0, 1,), 0)
-        do_motion(7, (0, 1,), 1)
+        do_motion(6, (0, 1,), 2)
+        do_motion(7, (0, 1,), 3)
         do_gain(3, nc.gpsimd)
         do_mul(6)
         do_mul(7)
-        turn(4, aa[4], None, True)
-        turn(5, sh[5], 3, False)
-        turn(5, aa[5], None, True)
+        turn(4, aa[4], 0, True)
+        turn(5, aa[5], 1, True)
         turn(6, sh[6], 4, False)
         turn(6, aa[6], None, True)
         turn(7, sh[7], 5, False)
@@ -461,6 +482,6 @@ def tile_list_gait_breed_grading_kernel(tc, tab_words, tab_scales, tab2_words, t
         do_quant(6)
         do_out(1, 1, 7, nc.scalar)
         do_gain(7, nc.vector)
-        do_out(2, 1, 2, nc.scalar)
+        do_out(2, 1, 0, nc.scalar)
         do_quant(7)
-        do_last_out(3, 0, 1)
+        do_last_out(3, 2, 3)

@@ -425,13 +425,12 @@ def tile_list_gait_breed_grading_kernel(tc, tab_words, tab_scales, tab2_words, t
         do_motion(0, (0,), 0)
         do_motion(1, (0,), 1)
         do_motion(2, (0,), 2)
-        do_motion(3, (0,), 3)
         gather_words(1, 0, 2)
         gather_words(1, 2, 4)
         do_motion(0, (1,))
         do_motion(1, (1,))
         do_motion(2, (1,))
-        do_motion(3, (1,))
+        do_motion(3, (1, 0,), 3)
         do_mul(0)
         do_mul(1)
         do_mul(2)
@@ -444,25 +443,25 @@ def tile_list_gait_breed_grading_kernel(tc, tab_words, tab_scales, tab2_words, t
         do_silu(1)
         do_motion(5, (0, 1,), 1)
         do_mul(4)
-        add_shift(4, nc.vector)
         quantise_w4(0)
-        do_gain(0, nc.gpsimd)
+        do_gain(0, nc.vector)
         do_mul(5)
         turn(2, aa[2], None, True)
+        turn(4, sh[4], 2, False)
         turn(3, aa[3], None, True)
         do_silu(2)
         do_silu(3)
         round_w4(1, nc.scalar, "aa3")
-        add_shift(5, nc.vector)
         do_gain(1, nc.vector)
         do_gain(2, nc.vector)
-        do_motion(6, (0, 1,), 2)
-        do_motion(7, (0, 1,), 3)
+        do_motion(6, (0, 1,), 0)
+        do_motion(7, (0, 1,), 1)
         do_gain(3, nc.gpsimd)
         do_mul(6)
         do_mul(7)
-        turn(4, aa[4], 0, True)
-        turn(5, aa[5], 1, True)
+        turn(4, aa[4], None, True)
+        turn(5, sh[5], 3, False)
+        turn(5, aa[5], None, True)
         turn(6, sh[6], 4, False)
         turn(6, aa[6], None, True)
         turn(7, sh[7], 5, False)
@@ -482,6 +481,6 @@ def tile_list_gait_breed_grading_kernel(tc, tab_words, tab_scales, tab2_words, t
         do_quant(6)
         do_out(1, 1, 7, nc.scalar)
         do_gain(7, nc.vector)
-        do_out(2, 1, 0, nc.scalar)
+        do_out(2, 1, 2, nc.scalar)
         do_quant(7)
-        do_last_out(3, 2, 3)
+        do_last_out(3, 0, 1)

@@ -456,7 +456,7 @@ def tile_list_gait_breed_grading_kernel(tc, tab_words, tab_scales, tab2_words, t
         do_gain(2, nc.vector)
         do_motion(6, (0, 1,), 0)
         do_motion(7, (0, 1,), 1)
-        do_gain(3, nc.gpsimd)
+        do_gain(3, nc.vector)
         do_mul(6)
         do_mul(7)
         turn(4, aa[4], None, True)

@@ -144,8 +144,8 @@ def tile_list_gait_breed_grading_kernel(tc, tab_words, tab_scales, tab2_words, t
                 nc.gpsimd.tensor_scalar(out=dst, in0=raw.rearrange("p t c -> p c t"), scalar1=1.0, scalar2=0.0,
                                         op0=ALU.mult, op1=ALU.add)
                 return
-            d = dst.rearrange("p (c i) t -> p c t i", i=4)
-            s = raw.rearrange("p t (c i) -> p c t i", i=4)
+            d = dst.rearrange("p (c i) t -> p c t i", i=2)
+            s = raw.rearrange("p t (c i) -> p c t i", i=2)
             if eng is nc.scalar:
                 nc.scalar.copy(out=d, in_=s)
             else:

from contextlib import ExitStack

import concourse.mybir as mybir
from concourse.masks import make_identity

T, T2, S, K, K2, H, N = 2048, 1024, 512, 1024, 512, 1024, 256
FLOPS = 2 * S * (K * H + 2 * K2 * H + H * N)

F32 = mybir.dt.float32
BF16 = mybir.dt.bfloat16
I32 = mybir.dt.int32
U32 = mybir.dt.uint32
U16 = mybir.dt.uint16
U8 = mybir.dt.uint8
FP8X4 = mybir.dt.float8_e4m3fn_x4
FP4X4 = mybir.dt.float4_e2m1fn_x4
ACT = mybir.ActivationFunctionType
ALU = mybir.AluOpType

P = 128
PACK = 4
KP = P * PACK
JC = 128
CHUNKS = S // JC
HALVES = H // KP
QW = KP // 2


def tile_list_gait_breed_grading_kernel(tc, tab_words, tab_scales, tab2_words, tab2_scales, offs, offs2,
                                                 w1_words, w1_scales, w2, w3_words, w3_scales, gain, w4, out):
    nc = tc.nc
    with ExitStack() as ctx:
        keep = ctx.enter_context(tc.tile_pool(name="keep", bufs=1))
        shared = ctx.enter_context(tc.tile_pool(name="shared", bufs=1))
        psum = ctx.enter_context(tc.psum_pool(name="psum", bufs=1))

        def bank_tile(shape, name, bank):
            return psum.tile(shape, F32, name=name, tag=f"bank{bank}")

        def held(shape, dtype, name, tag=None):
            if isinstance(tag, int):
                return shared.tile(shape, dtype, name=name, offset=tag, align_bytes=64)
            return keep.tile(shape, dtype, name=name, tag=tag or name, align_bytes=64)

        list1 = held([P, S // 16], U16, "list1")
        list2 = held([P, S // 16], U16, "list2")
        tab2w = held([P, T2], U16, "tab2w")
        tab2s = held([P, 1, T2], U8, "tab2s")
        tabw = [held([P, T], U32, "tabw0"), held([P, T], U32, "tabw1")]
        tabs = held([P, T], U8, "tabs", 8128)
        vs = {1: held([P, S], U8, "vs1")}
        w1s = held([P, 2, H], U8, "w1s")
        w3s = held([P, 1, H], U8, "w3s")
        warm = held([P, 2], F32, "warm")
        ident = held([P, P], F32, "ident")
        gains = held([P, HALVES, PACK], F32, "gains", 9344)
        w3c = held([P, H], I32, "w3c")
        w2raw, w1c, w1p, w4raw = {}, {}, {}, {}

        nc.vector.memset(tab2s[:, 0, :].bitcast(I32), 0)
        nc.vector.memset(warm[:, 0:1], 0.0)
        nc.scalar.activation(out=warm[:, 1:2], in_=warm[:, 0:1], func=ACT.Silu)
        nc.vector.memset(w3s[:, 0, :].bitcast(I32), 0)
        nc.vector.memset(tabs[:].bitcast(I32), 0)
        nc.vector.memset(w1s[:].rearrange("p a n -> p (a n)").bitcast(I32), 0)
        nc.vector.memset(vs[1][:].bitcast(I32), 0)

        def load_w2(q, tag=None):
            w2raw[q] = held([P, PACK, QW], F32, f"w2raw{q}", tag)
            nc.sync.dma_start(out=w2raw[q][:], in_=w2[:, q * QW:(q + 1) * QW].rearrange("(p j) c -> p j c", j=PACK))

        def load_w2_half(b, tag=None):
            both = held([P, PACK, KP], F32, f"w2half{b}", tag)
            nc.sync.dma_start(out=both[:], in_=w2[:, b * KP:(b + 1) * KP].rearrange("(p j) c -> p j c", j=PACK))
            w2raw[2 * b] = both[:, :, 0:QW]
            w2raw[2 * b + 1] = both[:, :, QW:KP]

        def load_w2_rows(pair):
            if not w2raw:
                whole = held([P, PACK, H], F32, "w2whole")
                w2raw["whole"] = whole
                for q in range(H // QW):
                    w2raw[q] = whole[:, :, q * QW:(q + 1) * QW]
            rows = slice(2 * pair, 2 * pair + 2)
            nc.sync.dma_start(out=w2raw["whole"][:, rows, :], in_=w2.rearrange("(p j) c -> p j c", j=PACK)[:, rows, :])

        def load_w1_pass(a, tag=None):
            w1p[a] = held([P, H // 2], I32, f"w1p{a}", tag)
            nc.sync.dma_start(out=w1p[a][:], in_=w1_words[a].bitcast(I32))

        w1q = {}

        def load_w1_piece(a, b, tag=None):
            w1q[a, b] = held([P, QW], I32, f"w1q{a}{b}", tag)
            nc.sync.dma_start(out=w1q[a, b][:], in_=w1_words[a][:, 2 * KP * b:2 * KP * (b + 1)].bitcast(I32))

        def load_w1(b, tag=None):
            w1c[b] = held([P, 2, KP // 2], I32, f"w1c{b}", tag)
            nc.sync.dma_start(out=w1c[b][:],
                              in_=w1_words.rearrange("a p n -> p a n")[:, :, 2 * KP * b:2 * KP * (b + 1)].bitcast(I32))

        def load_w4(b, tag=None):
            if not w4raw:
                both = held([P, HALVES, PACK, N], F32, "w4raw", tag)
                for half in range(HALVES):
                    w4raw[half] = both[:, half]
            nc.sync.dma_start(out=w4raw[b], in_=w4[b * KP:(b + 1) * KP, :].rearrange("(p t) n -> p t n", t=PACK))

        def load_tab(a):
            nc.sync.dma_start(out=tabw[a][:].bitcast(I32), in_=tab_words[a].rearrange("p n t -> p (n t)").bitcast(I32))

        def scale_rows(plane, scales):
            for r in range(4):
                rows = scales[:, r:16:4, :].rearrange("a q n -> q a n").bitcast(I32)
                nc.sync.dma_start(out=plane[r:P:32].bitcast(I32), in_=rows)

        def load_tabs():
            for r in range(4):
                nc.sync.dma_start(out=tabs[r:P:16].bitcast(I32),
                                  in_=tab_scales[:, r:16:4, :].rearrange("a q n -> q a n").bitcast(I32))

        def load_tab2w():
            nc.sync.dma_start(out=tab2w[:].bitcast(I32), in_=tab2_words[0].bitcast(I32))

        def load_w3():
            nc.sync.dma_start(out=w3c[:], in_=w3_words[0].rearrange("p n t -> p (n t)").bitcast(I32))

        def load_gain():
            nc.sync.dma_start(out=gains[:], in_=gain.rearrange("(b p t) -> p b t", p=P, t=PACK))

        def move_rows():
            for r in range(4):
                nc.sync.dma_start(out=vs[1][r:P:32].bitcast(I32), in_=vs[0][16 + r:P:32].bitcast(I32))

        v2w = held([P, S], U16, "v2w")
        v2s = held([P, S], U8, "v2s")
        vw = {}

        def cols(c):
            return slice(c * JC, (c + 1) * JC)

        def weave(eng, dst, raw):
            if eng is nc.gpsimd:
                nc.gpsimd.tensor_scalar(out=dst, in0=raw.rearrange("p t c -> p c t"), scalar1=1.0, scalar2=0.0,
                                        op0=ALU.mult, op1=ALU.add)
                return
            d = dst.rearrange("p (c i) t -> p c t i", i=2)
            s = raw.rearrange("p t (c i) -> p c t i", i=2)
            if eng is nc.scalar:
                nc.scalar.copy(out=d, in_=s)
            else:
                nc.vector.tensor_copy(out=d, in_=s)

        w2g, w4g = {}, {}
        w2c = [held([P, KP], U32, f"w2c{b}") for b in range(HALVES)]
        w2s = [held([P, KP], U8, f"w2s{b}") for b in range(HALVES)]

        def round_w2(q, eng, tag=None, lo=0, hi=QW):
            b = q // 2
            if b not in w2g:
                w2g[b] = held([P, KP, PACK], BF16, f"w2g{b}", tag)
            first = (q % 2) * QW
            weave(eng, w2g[b][:, first + lo:first + hi], w2raw[q][:, :, lo:hi])

        def quantise_w2(b):
            nc.vector.quantize_mx(out=w2c[b][:].bitcast(FP8X4), scales=w2s[b][:], in_=w2g[b][:].rearrange("p c t -> p (c t)"))

        w2q = {}

        def quantise_quarter(q):
            w2q[q] = (held([P, QW], U32, f"w2qc{q}"), held([P, QW], U8, f"w2qs{q}"))
            nc.vector.quantize_mx(out=w2q[q][0][:].bitcast(FP8X4), scales=w2q[q][1][:],
                                  in_=w2r[q][:].rearrange("p c t -> p (c t)"))

        w2r = {}

        def round_quarter(q, eng, tag=None):
            w2r[q] = held([P, QW, PACK], BF16, f"w2r{q}", tag)
            weave(eng, w2r[q][:], w2raw[q][:])

        pair_bank, pair_th = {}, {}

        def scale_pair(u, q, bank):
            pair_bank[u, q] = bank_tile([P, 2, QW], f"scale{u}q{q}", bank)
            for i in range(2):
                c = units[u + i][1]
                nc.tensor.matmul_mx(out=pair_bank[u, q][:, i, :], lhsT=v2w[:, cols(c)].bitcast(FP4X4), lhsT_scale=v2s[:, cols(c)],
                                    rhs=w2q[q][0][:].bitcast(FP8X4), rhs_scale=w2q[q][1][:], start=True, stop=True)

        def tanh_pair(u, q):
            if u not in pair_th:
                pair_th[u] = held([P, 2, PACK, P], F32, f"thp{u}")
                for i in range(2):
                    th[u + i] = pair_th[u][:, i]
            half = slice((q % 2) * P // 2, (q % 2 + 1) * P // 2)
            nc.scalar.activation(out=pair_th[u][:, :, :, half], in_=pair_bank[u, q][:].rearrange("p i (q t) -> p i t q", t=PACK),
                                 func=ACT.Tanh)

        def gather_scales(tag=None):
            vs[0] = held([P, S], U8, "vs0", tag)
            nc.vector.tensor_copy(out=vs[0][:], in_=tabs[:].indirect(list1[:]))

        def gather_words(a, lo, hi, tag=None):
            tile = held([P, (hi - lo) * JC], U32, f"vw{a}{lo}", tag)
            nc.vector.tensor_copy(out=tile[:], in_=tabw[a][:].indirect(list1[:, 8 * lo:8 * hi]))
            for c in range(lo, hi):
                vw[a, c] = tile[:, cols(c - lo)]

        units = [(b, c) for b in range(HALVES) for c in range(CHUNKS)]
        groups = [(0, 4), (4, 5), (5, 6), (6, 7), (7, 8)]
        th, sh, xt, ss, hb, mo, aa, sc, sp = {}, {}, {}, {}, {}, {}, {}, {}, {}
        hc, hs, hw, begun = {}, {}, {}, {}

        def planes(bank):
            return bank[:].rearrange("p (q t) -> p t q", t=PACK)

        def do_scale(u, bank):
            b, c = units[u]
            sc[u] = bank_tile([P, KP], f"scale{u}", bank)
            nc.tensor.matmul_mx(out=sc[u][:], lhsT=v2w[:, cols(c)].bitcast(FP4X4), lhsT_scale=v2s[:, cols(c)],
                                rhs=w2c[b][:].bitcast(FP8X4), rhs_scale=w2s[b][:], start=True, stop=True)

        def do_tanh(u, tag=None):
            th[u] = held([P, PACK, P], F32, f"th{u}", tag)
            nc.scalar.activation(out=th[u][:], in_=planes(sc[u]), func=ACT.Tanh)

        def do_shift(u, bank):
            b, c = units[u]
            sp[u] = bank_tile([P, KP], f"shift{u}", bank)
            nc.tensor.matmul_mx(out=sp[u][:], lhsT=v2w[:, cols(c)].bitcast(FP4X4), lhsT_scale=v2s[:, cols(c)],
                                rhs=w3c[:, b * KP:(b + 1) * KP].bitcast(FP8X4), rhs_scale=w3s[:, 0, b * KP:(b + 1) * KP],
                                start=True, stop=True)

        def copy_shift(u, eng, tag=None):
            sh[u] = held([P, PACK, P], F32, f"sh{u}", tag)
            if eng is nc.scalar:
                nc.scalar.copy(out=sh[u][:], in_=planes(sp[u]))
            else:
                nc.vector.tensor_copy(out=sh[u][:], in_=planes(sp[u]))

        def turn(u, src, bank, last):
            opens = u not in xt
            if opens:
                xt[u] = bank_tile([P, PACK, JC], f"xt{u}", bank)
            for t in range(PACK):
                nc.tensor.matmul(xt[u][:, t, :], src[:, t, :], ident[:], start=(opens and t == 0),
                                 stop=(last and t == PACK - 1), is_transpose=True)

        def do_motion(u, passes, bank=None):
            b, c = units[u]
            if u not in mo:
                mo[u] = bank_tile([P, KP], f"motion{u}", bank)
            for a in passes:
                nc.tensor.matmul_mx(out=mo[u][:], lhsT=vw[a, c].bitcast(FP8X4), lhsT_scale=vs[a][:, cols(c)],
                                    rhs=(w1c[b][:, a, :] if b else w1q[a, b][:]).bitcast(FP4X4), rhs_scale=w1s[:, a, b * KP:(b + 1) * KP],
                                    start=(u not in begun), stop=(u in begun))
                begun[u] = True

        def do_mul(u, tag=None):
            aa[u] = held([P, PACK, P], F32, f"aa{u}", tag)
            for ts in ([slice(0, 2), slice(2, 4)] if u == len(units) - 1 else [slice(0, PACK)]):
                nc.vector.scalar_tensor_tensor(out=aa[u][:, ts], in0=th[u][:, ts], scalar=1.0, in1=planes(mo[u])[:, ts],
                                               op0=ALU.add, op1=ALU.mult)

        def add_shift(u, eng, tag=None):
            total = held([P, PACK, P], F32, f"sum{u}", tag)
            eng.tensor_tensor(out=total[:], in0=aa[u][:], in1=sh[u][:], op=ALU.add)
            aa[u] = total

        def parts(u):
            return [slice(0, JC // 2), slice(JC // 2, JC)] if u == len(units) - 1 else [slice(0, JC)]

        def do_silu(u, tag=None):
            ss[u] = held([P, JC, PACK], F32, f"ss{u}", tag)
            for js in parts(u):
                nc.scalar.activation(out=ss[u][:, js], in_=xt[u][:].rearrange("p t j -> p j t")[:, js], func=ACT.Silu)

        def do_gain(u, eng, tag=None):
            b, c = units[u]
            for lo, hi in groups:
                if lo <= u < hi:
                    if lo not in hw:
                        hw[lo] = held([P, (hi - lo) * JC, PACK], BF16, f"hb{lo}", tag)
                    hb[u] = hw[lo][:, (u - lo) * JC:(u - lo + 1) * JC, :]
            for js in parts(u):
                eng.tensor_tensor(out=hb[u][:, js], in0=ss[u][:, js],
                                  in1=gains[:, b, :].unsqueeze(1).to_broadcast([P, js.stop - js.start, PACK]), op=ALU.mult)

        def group_tile(u, tag=None):
            for lo, hi in groups:
                if lo <= u < hi:
                    if lo not in hw:
                        hw[lo] = held([P, (hi - lo) * JC, PACK], BF16, f"hb{lo}", tag)
                    return hw[lo][:, (u - lo) * JC:(u - lo + 1) * JC, :]

        def silu_planes(u, tag=None):
            ss[u] = held([P, PACK, JC], F32, f"ss{u}", tag)
            nc.scalar.activation(out=ss[u][:], in_=xt[u][:], func=ACT.Silu)

        def gain_planes(u, tag=None):
            b, c = units[u]
            hb[u] = held([P, PACK, JC], BF16, f"hp{u}", tag)
            for t in range(PACK):
                nc.scalar.activation(out=hb[u][:, t, :], in_=ss[u][:, t, :], func=ACT.Copy, scale=gains[:, b, t:t + 1])

        def weave_h(u, tag=None):
            weave(nc.vector, group_tile(u, tag), hb[u][:])

        def do_quant(lo, tag=None):
            hi = dict(groups)[lo]
            codes = held([P, (hi - lo) * JC], U32, f"hc{lo}", tag)
            plane = held([P, (hi - lo) * JC], U8, f"hs{lo}")
            for u in range(lo, hi):
                hc[units[u]] = (codes, (u - lo) * JC)
                hs[units[u]] = plane
            nc.vector.quantize_mx(out=codes[:].bitcast(FP8X4), scales=plane[:], in_=hw[lo][:].rearrange("p j t -> p (j t)"))

        w4s, w4c = {}, {}

        def round_w4(b, eng, tag=None):
            w4g[b] = held([P, N, PACK], BF16, f"w4g{b}", tag)
            weave(eng, w4g[b][:], w4raw[b])

        def quantise_w4(b, tag=None):
            w4c[b] = held([P, N], U32, f"w4c{b}", tag)
            w4s[b] = held([P, N], U8, f"w4s{b}")
            nc.vector.quantize_mx(out=w4c[b][:].bitcast(FP8X4), scales=w4s[b][:], in_=w4g[b][:].rearrange("p n t -> p (n t)"))

        def out_pass(dst, b, h, c, width, start, stop):
            codes, first = hc[b, c]
            nc.tensor.matmul_mx(out=dst, lhsT=w4c[b][:, h * P:(h + 1) * P].bitcast(FP8X4), lhsT_scale=w4s[b][:, h * P:(h + 1) * P],
                                rhs=codes[:, first:first + width].bitcast(FP8X4), rhs_scale=hs[b, c][:, first:first + width],
                                start=start, stop=stop)

        def do_last_out(c, bank0, bank1):
            banks = [bank_tile([P, JC], "last0", bank0), bank_tile([P, JC], "last1", bank1)]
            for b in range(HALVES):
                for h in range(N // P):
                    out_pass(banks[h][:], b, h, c, JC, b == 0, b == HALVES - 1)
            res = [held([P, JC], F32, f"last{h}") for h in range(N // P)]
            nc.vector.tensor_copy(out=res[0][:], in_=banks[0][:])
            nc.sync.dma_start(out=out[0:P, cols(c)], in_=res[0][:])
            nc.scalar.copy(out=res[1][:], in_=banks[1][:])
            nc.scalar.dma_start(out=out[P:2 * P, cols(c)], in_=res[1][:])

        def do_out(c, chunks, bank, eng):
            width = chunks * JC
            acc = bank_tile([P, N // P, width], f"out{c}", bank)
            for b in range(HALVES):
                for h in range(N // P):
                    out_pass(acc[:, h, :], b, h, c, width, b == 0 and h == 0, b == HALVES - 1 and h == N // P - 1)
            res = held([P, N // P, width], F32, f"res{c}")
            if eng is nc.scalar:
                nc.scalar.copy(out=res[:], in_=acc[:])
            else:
                nc.vector.tensor_copy(out=res[:], in_=acc[:])
            nc.sync.dma_start(out=out.rearrange("(h p) j -> p h j", p=P)[:, :, c * JC:c * JC + width], in_=res[:])

        load_tab2w()
        nc.sync.dma_start(list2[:], offs2)
        scale_rows(tab2s[:], tab2_scales)
        load_w3()
        load_w2_half(0)
        scale_rows(w3s[:], w3_scales)
        nc.sync.dma_start(list1[:], offs)
        load_w2_half(1)
        load_tabs()
        load_tab(0)
        load_w1_piece(0, 0)
        scale_rows(w1s[:], w1_scales)
        load_tab(1)
        load_w1_piece(1, 0)
        make_identity(nc, ident[:])
        nc.vector.tensor_copy(out=v2w[:], in_=tab2w[:].indirect(list2[:]))
        nc.vector.tensor_copy(out=v2s[:], in_=tab2s[:, 0, :].indirect(list2[:]))
        round_w2(0, nc.vector)
        round_w2(1, nc.vector)
        quantise_w2(0)
        do_shift(0, 0)
        do_shift(1, 1)
        do_shift(2, 2)
        do_shift(3, 3)
        do_shift(4, 4)
        do_shift(5, 5)
        do_shift(6, 6)
        do_shift(7, 7)
        copy_shift(0, nc.scalar)
        copy_shift(1, nc.scalar)
        copy_shift(2, nc.scalar)
        copy_shift(3, nc.scalar)
        copy_shift(4, nc.scalar)
        copy_shift(5, nc.scalar)
        copy_shift(6, nc.scalar)
        copy_shift(7, nc.scalar)
        do_scale(0, 0)
        do_scale(1, 1)
        do_scale(2, 2)
        do_scale(3, 3)
        do_tanh(0)
        do_tanh(1)
        do_tanh(2)
        do_tanh(3)
        turn(0, sh[0], 4, False)
        turn(1, sh[1], 5, False)
        turn(2, sh[2], 6, False)
        turn(3, sh[3], 7, False)
        round_w2(2, nc.vector)
        round_w2(3, nc.vector)
        quantise_w2(1)
        gather_scales("w2g1")
        move_rows()
        load_w1(1, 10112)
        load_w4(0, 0)
        load_gain()
        load_w4(1)
        do_scale(4, 0)
        do_scale(5, 1)
        do_scale(6, 2)
        do_scale(7, 3)
        do_tanh(4)
        do_tanh(5)
        do_tanh(6)
        do_tanh(7)
        gather_words(0, 0, 4, "w2g0")
        do_motion(0, (0,), 0)
        do_motion(1, (0,), 1)
        do_motion(2, (0,), 2)
        gather_words(1, 0, 2)
        gather_words(1, 2, 4)
        do_motion(0, (1,))
        do_motion(1, (1,))
        do_motion(2, (1,))
        do_motion(3, (1, 0,), 3)
        do_mul(0)
        do_mul(1)
        do_mul(2)
        do_mul(3)
        do_motion(4, (0, 1,), 0)
        turn(0, aa[0], None, True)
        turn(1, aa[1], None, True)
        round_w4(0, nc.scalar)
        do_silu(0)
        do_silu(1)
        do_motion(5, (0, 1,), 1)
        do_mul(4)
        quantise_w4(0)
        do_gain(0, nc.vector)
        do_mul(5)
        turn(2, aa[2], None, True)
        turn(4, sh[4], 2, False)
        turn(3, aa[3], None, True)
        do_silu(2)
        do_silu(3)
        round_w4(1, nc.scalar, "aa3")
        do_gain(1, nc.vector)
        do_gain(2, nc.vector)
        do_motion(6, (0, 1,), 0)
        do_motion(7, (0, 1,), 1)
        do_gain(3, nc.vector)
        do_mul(6)
        do_mul(7)
        turn(4, aa[4], None, True)
        turn(5, sh[5], 3, False)
        turn(5, aa[5], None, True)
        turn(6, sh[6], 4, False)
        turn(6, aa[6], None, True)
        turn(7, sh[7], 5, False)
        turn(7, aa[7], None, True)
        do_silu(4)
        do_silu(5)
        do_silu(6)
        do_silu(7)
        quantise_w4(1)
        do_quant(0)
        do_gain(4, nc.vector)
        do_gain(5, nc.vector)
        do_quant(4)
        do_gain(6, nc.vector)
        do_quant(5)
        do_out(0, 1, 6, nc.scalar)
        do_quant(6)
        do_out(1, 1, 7, nc.scalar)
        do_gain(7, nc.vector)
        do_out(2, 1, 2, nc.scalar)
        do_quant(7)
        do_last_out(3, 0, 1)
